import numpy as np, ml_dtypes
CORES = [25,29,65,69,153,157,193,197]
N = 8
import mx_ref
BF = ml_dtypes.bfloat16
def gentries(a):
    return np.ascontiguousarray(a.reshape(8, 16, -1).transpose(0, 2, 1)).reshape(8, -1)
def gtable(e):
    e = np.asarray(e); return np.ascontiguousarray(e.reshape(8, -1, 16).transpose(0, 2, 1)).reshape(128, -1).astype(np.int32)
def gcols(t, e):
    v = np.concatenate([t.reshape(8, 16, -1, 4), np.zeros((8, 16, 1, 4), BF)], axis=2)
    return np.ascontiguousarray(np.stack([v[g][:, e[g]] for g in range(8)])).reshape(128, -1)
def tile(rs):
    return np.stack(rs, axis=2).reshape(128, -1).astype(BF)
def cut(t, i, w=512):
    return t[:, w * i:w * i + w]
def pick(q, e):
    c = np.concatenate([q[0].reshape(128, -1, 4), np.zeros((128, 1, 4), np.uint8)], axis=1); s = np.concatenate([q[1], np.ones((16, 1), np.uint8)], axis=1)
    return (np.ascontiguousarray(c[:, e].reshape(128, -1)), np.ascontiguousarray(s[:, e]))
def join(*qs):
    return (np.concatenate([q[0] for q in qs], axis=1), np.concatenate([q[1] for q in qs], axis=1))
def put(q, e, v):
    c, s = q[0].reshape(128, -1, 4).copy(), q[1].copy(); c[:, e] = v[0].reshape(128, -1, 4); s[:, e] = v[1]
    return (c.reshape(128, -1), s)
def pk(c, s):
    return (np.ascontiguousarray(c), mx_ref.live(s))
def emit(q):
    return q[0], q[1]
def packed(v, rng):
    q = [mx_ref.quantize(np.ascontiguousarray(v[r])) for r in range(N)]
    return np.stack([a for a, b in q]), np.stack([mx_ref.plane(b, rng) for a, b in q])
def values_of_codes():
    e, c = np.zeros((128, 128, 4), np.float32), np.zeros((128, 2, 4), np.uint8)
    e[np.arange(128), np.arange(128), 0] = 1
    c[:127, :, 0] = np.arange(256).reshape(2, 128).T[:127]
    return mx_ref.matmul(mx_ref.quantize(e.reshape(128, 512).astype(BF)), (c.reshape(128, 8), np.full((16, 2), 127, np.uint8))).T.reshape(-1).astype(np.float64)
CODE_VALUE, SCALE_VALUE = values_of_codes(), 2.0 ** (np.arange(256) - 127.0)
def decode(q):
    return (CODE_VALUE[q[0]].reshape(16, 8, -1, 4) * SCALE_VALUE[q[1]][:, None, :, None] + 0.0).reshape(128, -1).astype(np.float32)
def f(rng, *shape):
    return mx_ref.flush((rng.standard_normal(shape, dtype=np.float32) * np.exp2(rng.integers(-2, 3, shape[:-1] + (1,)))).astype(BF))
def wide(rng, *shape, cols=0):
    v = rng.standard_normal(shape, dtype=np.float32) * np.exp2(rng.integers(-12, 13, shape)).astype(np.float32)
    if cols: v *= np.repeat(np.exp2(rng.integers(-cols, cols + 1, shape[:-2] + (1, shape[-1] // 4))) * (rng.random(shape[:-2] + (1, shape[-1] // 4)) > 0.0625), 4, axis=-1).astype(np.float32)
    return mx_ref.flush(v.astype(BF))
C, K, A, R = 352, 96, 320, 3
def big(v):
    v = v.astype(np.float32)
    v[np.abs(v) < np.float32(2.0 ** -16)] = 0
    return v.astype(BF)
def numbers_of(rng):
    return {"x": big(f(rng, N, 128, 4 * C)), "u": np.array(f(rng, N, 128, 512)), "v": np.array(f(rng, N, 128, 512))}
def weights(rng, w):
    c, p = packed(w, rng)
    return {"wc": c, "ws": p}
def still(rng):
    w = np.zeros((N, 128, 4, 128, 4), np.float32)
    i = np.arange(128)
    for b in range(4): w[:, i, b, i, b] = 32
    return weights(rng, w.reshape(N, 128, 2048).astype(BF))
def clauses(rng):
    return rng.integers(0, C + K, (N, 8, A, 4))
def stored(l):
    return {"cl": np.stack([gtable(e) for e in l])}
def signs(rng):
    return np.stack([rng.permutation(8) % 2 * 2.0 - 1.0 for r in range(N)])
def setup_inputs(rng):
    return {**numbers_of(rng), **stored(clauses(rng)), **weights(rng, f(rng, N, 128, 2048))}
def setup_inputs_signs(rng):
    d = numbers_of(rng)
    o = rng.permutation(N)
    kinds = np.array([[0, 0, -1, -2, 1, 1, 1, 2], [0, 0, 0, -1, -1, -2, 1, 2], [0, -1, -1, -2, -2, -2, -1, -1], [1, 1, 1, 1, 2, 2, 1, 1]])
    small = rng.permutation(N) % 2 == 0
    x = d["x"].reshape(N, 8, 16, C, 4)
    u = d["u"].reshape(N, 128, 128, 4)
    x[:, :, :8] = 0
    u[:, :, ::16] = 0
    for r in range(N):
        i = rng.permuted(np.tile(np.arange(C) % 8, (8, 1)), axis=1)
        size = 2.0 ** -30 if small[r] else 1.0
        x[r, :, 0, :, 0] = ((12 + kinds[o[r] % 4][i]) * size).astype(np.float32).astype(BF)
        x[r, :, 0, :, 1] = 12 * size
        for h in range(0, 128, 16):
            u[r, h, h, 0] = size
            u[r, h, h, 1] = -size
    return {"x": x.reshape(N, 128, 4 * C), "u": u.reshape(N, 128, 512), "v": d["v"], **stored(clauses(rng)), **still(rng)}
def setup_inputs_near(rng):
    d = numbers_of(rng)
    x = d["x"].astype(np.float32).reshape(N, 8, 16, C, 4)
    s = np.minimum((np.arange(C) + 1) // 2, 255)
    g = ((s[:, None] >> np.arange(8)) & 1) * np.exp2(np.arange(8) - 23.0)
    x[:, :, 0] = 0
    x[:, :, 0, :, 0] = signs(rng)[:, :, None]
    x[:, :, 8] = g[:, :4]
    x[:, :, 9] = g[:, 4:]
    x[:, :, 10:] = rng.integers(4, 8, (N, 8, 6, C, 4)) * rng.choice([-1.0, 1.0], (N, 8, 6, C, 4)) * 2.0 ** -20
    u = d["u"].reshape(N, 128, 128, 4)
    k = np.where(rng.permutation(N) < N // 2, 2.0 ** -30, 1.0).astype(np.float32).astype(BF)
    u[:, :, ::16] = 0
    for h in range(0, 128, 16):
        u[:, h, h, 0] = k
        u[:, h + 8:h + 10, h] = k[:, None, None]
    return {"x": x.reshape(N, 128, 4 * C).astype(BF), "u": u.reshape(N, 128, 512), "v": d["v"], **stored(clauses(rng)), **still(rng)}
def setup_inputs_huge(rng):
    d = numbers_of(rng)
    x = 2.0 ** 30 * (0.8 + 0.2 * rng.random((N, 128, C, 4)))
    c = np.stack([rng.permutation(C) % 2 * 2.0 - 1.0 for r in range(N)])
    o = rng.permutation(N)
    c[o < N // 2] = 1
    for r in range(N):
        if o[r] >= N - N // 4: c[r] = np.where(np.arange(C) % 4 == rng.integers(4), 1.0, -1.0)
    x *= c[:, None, :, None]
    u = d["u"].reshape(N, 128, 128, 4)
    a = 2.0 ** 30 * (1 - 0.1 * rng.random((N, 128, 8, 4))) * signs(rng)[:, None, :, None]
    u[:, :, ::16] = a.astype(np.float32).astype(BF)
    return {"x": x.astype(np.float32).reshape(N, 128, 4 * C).astype(BF), "u": u.reshape(N, 128, 512), "v": d["v"], **stored(clauses(rng)), **still(rng)}
def setup_inputs_lists(rng):
    d = numbers_of(rng)
    l = clauses(rng)
    o = rng.permutation(N)
    for r in range(N):
        if o[r] % 4 == 0: l[r] = C + (np.argsort(rng.random((8, A)), axis=1) % K)[:, :, None]
        if o[r] % 4 == 1: l[r] = rng.integers(0, C, (8, A, 4))
        if o[r] % 4 == 2: l[r] = C + rng.integers(0, K, (8, 1, 1))
        if o[r] % 4 == 3:
            l[r, :, :256] = rng.integers(0, C, (8, 256, 4))
            l[r, :, 256:] = rng.integers(C, C + K, (8, A - 256, 4))
    return {**d, **stored(l), **weights(rng, f(rng, N, 128, 2048))}
def setup_inputs_spread(rng):
    d = setup_inputs(rng)
    d["x"] = big(wide(rng, N, 128, 4 * C, cols=6))
    return d
def check_inputs(d):
    b = []
    for k in ("x", "u", "v"):
        a = np.abs(d[k].astype(np.float32))
        if not (np.isfinite(a).all() and ((a == 0) | (a >= 2.0 ** -30) & (a <= 2.0 ** 30)).all()): b.append("a value of " + k)
    if ((d["cl"] < 0) | (d["cl"] >= C + K)).any(): b.append("an entry of cl")
    return b
def mean(a, b):
    return ((a.astype(np.float32) + b.astype(np.float32)) * np.float32(0.5)).astype(BF)
def reference(x, u, v, cl, wc, ws):
    qu = [mx_ref.quantize(u[r]) for r in range(N)]
    lay = [pk(wc[r], ws[r]) for r in range(N)]
    lit = [gentries(cl[r]).reshape(8, A, 4).astype(np.int64) for r in range(N)]
    now = [x[r] for r in range(N)]
    cur = [np.zeros((8, A), np.int64) for r in range(N)]
    for t in range(R):
        own, e, sent, back = [], [], [], []
        for r in range(N):
            own.append(mx_ref.matmul(qu[r], mx_ref.quantize(now[r]))[::16] + np.float32(0.0))
            e.append(np.argsort(-own[r], axis=1, kind="stable")[:, :K])
            sent.append(mx_ref.quantize(gcols(now[r], e[r])))
        came = decode(join(*sent)).astype(BF)
        for r in range(N):
            p = (r - 1) % N
            place = np.concatenate([now[r], cut(came, p, 4 * K)], axis=1)
            yes = np.concatenate([own[r], mx_ref.matmul(qu[r], sent[p])[::16]], axis=1) > 0
            named = np.stack([yes[g][lit[r][g]] for g in range(8)])
            turn = (cur[r][:, :, None] + np.arange(4)) % 4
            cur[r] = (cur[r] + np.argmax(np.take_along_axis(named, turn, axis=2), axis=2)) % 4
            one = np.take_along_axis(lit[r], cur[r][:, :, None], axis=2)[:, :, 0]
            two = np.take_along_axis(lit[r], (cur[r][:, :, None] + 1) % 4, axis=2)[:, :, 0]
            q = mx_ref.quantize(mean(gcols(place, one), gcols(place, two)))
            h = tile([mx_ref.matmul(pick(lay[r], np.arange(128 * b, 128 * b + 128)), q) * np.float32(0.03125) for b in range(4)])
            first = np.full((8, C + K), -1)
            for j in range(A - 1, -1, -1): first[np.arange(8), one[:, j]] = j
            back.append(mx_ref.quantize(gcols(h, first[:, C:])))
        home = decode(join(*back)).astype(BF)
        for r in range(N):
            new = now[r].copy().reshape(8, 16, C, 4)
            got = cut(home, (r + 1) % N, 4 * K).reshape(8, 16, K, 4)
            for g in range(8): new[g][:, e[r][g]] = mean(new[g][:, e[r][g]], got[g])
            now[r] = new.reshape(128, 4 * C)
    y, ow = np.zeros((N, 128, C), np.float32), np.zeros((N, 8, A), np.float32)
    oc, osc = np.zeros((N, 128, 4 * C), np.uint8), np.zeros((N, 16, C), np.uint8)
    for r in range(N):
        q = mx_ref.quantize(now[r])
        y[r] = mx_ref.matmul(mx_ref.quantize(v[r]), q)
        ow[r] = cur[r]
        oc[r], osc[r] = emit(q)
    return {"y": y, "ow": ow, "oc": oc, "osc": osc}

@@ -1,0 +1,547 @@
+from concourse.mybir import dt, AluOpType, ActivationFunctionType
+
+C, K, A, R = 352, 96, 320, 3
+PW = C + K
+HW = 336
+FW = A + 1
+BIG = 1e29
+TILES = [[21, 20, 19], [18, 17, 16, 15], [14, 13, 12, 11], [10, 9, 8, 7], [6, 5, 4, 3], [2, 1]]
+TWID = [352, 288, 224, 160, 128, 128]
+TOFF = [sum(TWID[:i]) for i in range(6)]
+X4, U8 = "float8_e4m3fn_x4", "uint8"
+
+
+def _sb(n, d):
+    return ("sbuf", [128, n], d)
+
+
+SCRATCH = {
+    "X": _sb(4 * C, "bfloat16"), "qx": _sb(C, X4), "sx": _sb(C, U8),
+    "ub": _sb(512, "bfloat16"), "qu0": _sb(128, X4), "su0": _sb(128, U8), "qu": _sb(128, X4), "su": _sb(128, U8),
+    "vb": _sb(512, "bfloat16"), "qv": _sb(128, X4), "sv": _sb(128, U8),
+    "qw": _sb(512, X4), "sw": _sb(512, U8),
+    "cli": _sb(80, "int32"), "clu": _sb(80, "uint16"),
+    "pint": _sb(8, "int32"), "cf": _sb(16, "float32"), "uoi": _sb(40, "int32"), "uoff": _sb(40, "uint16"),
+    "idt": _sb(PW, "float32"), "j16": _sb(K, "float32"), "j4": _sb(16, "float32"), "k1": _sb(K, "float32"),
+    "sm": _sb(96, "float32"), "rr": _sb(22, "uint16"), "eb": _sb(516, "bfloat16"),
+    "ab": _sb(512, "bfloat16"), "a0b": _sb(512, "bfloat16"), "zb": _sb(516, "bfloat16"),
+    "qa": _sb(256, X4), "sa": _sb(256, U8), "qe": _sb(512, X4), "se": _sb(512, U8),
+    "msel": _sb(C, "float32"), "mres": _sb(C, "float32"), "kr": _sb(C, "float32"), "ktm": _sb(K, "float32"),
+    "ktn": _sb(K, "float32"), "kt": _sb(1280, "bfloat16"), "ke": _sb(K, "float32"), "val": _sb(C, "float32"),
+    "cnt": _sb(22, "float32"), "kw": _sb(PW, "bfloat16"), "f0": _sb(6 * FW, "bfloat16"),
+    "gf": _sb(1280, "float32"), "sl": _sb(1280, "float32"), "li": _sb(80, "int32"), "loff": _sb(80, "uint16"),
+    "pay": _sb(80, "float32"), "pt": _sb(80, "float32"), "cur": _sb(20, "int32"), "wi": _sb(80, "int32"),
+    "wj": _sb(80, "int32"), "base": _sb(80, "float32"),
+    "t1": _sb(C, "float32"), "ex": _sb(C, "float32"), "ct": _sb(4 * 1280, "bfloat16"),
+    "qc": _sb(1280, X4), "sc": _sb(1280, U8), "sg": _sb(3 * C, "bfloat16"), "junk": _sb(2752, "bfloat16"),
+    "rs": _sb(22, "float32"), "rs1": _sb(22, "float32"), "rs2": _sb(22, "float32"), "cs": _sb(C, "float32"),
+    "ru": _sb(22, "float32"), "roff": _sb(22, "uint16"), "win": _sb(C, "float32"), "es": _sb(K, "float32"),
+    "eoff": _sb(24, "uint16"), "E": _sb(512, "bfloat16"), "eh": _sb(4 * K, "bfloat16"),
+    "qs": _sb(6 * 128, X4), "ss": _sb(6 * 128, U8), "ql": _sb(128 + 6 * K, X4), "sld": _sb(128 + 6 * K, U8),
+    "ph": _sb(4 * PW, "bfloat16"), "tw": _sb(PW, "bfloat16"), "tg": _sb(1280, "bfloat16"), "ts": _sb(1280, "bfloat16"),
+    "key": _sb(80, "float32"), "m1": _sb(40, "float32"), "mi": _sb(20, "int32"), "oti": _sb(40, "int32"),
+    "ooff": _sb(40, "uint16"), "za": _sb(1280, "bfloat16"), "Z": _sb(1280, "bfloat16"), "qz": _sb(A, X4), "sz": _sb(A, U8),
+    "H": _sb(4 * HW, "bfloat16"), "kg": _sb(A, "bfloat16"), "mk": _sb(6 * FW, "bfloat16"), "fs": _sb(6 * FW, "bfloat16"),
+    "foff": _sb(6, "uint16"), "V": _sb(512, "bfloat16"), "upd": _sb(4 * K, "bfloat16"),
+    "cw": _sb(32, "float32"), "cwt": _sb(32, "float32"), "yb": _sb(C, "float32"),
+}
+for _b in range(8):
+    SCRATCH["p%d" % _b] = ("psum", [128, 512], "float32")
+NDMA = 24
+SEMAPHORES = (["eV", "eA", "eT", "eG", "snt"] + ["arr%d" % _s for _s in range(6)] + ["d%d" % _s for _s in range(NDMA)])
+
+OP, AF = AluOpType, ActivationFunctionType
+
+
+def v(name, a, b, s=1):
+    return (name, a, b, s)
+
+
+def ind(win, off):
+    return ("*", win, off)
+
+
+def bits(x):
+    m = 0
+    if x[3] == 1:
+        return ((1 << (x[2] - x[1])) - 1) << x[1]
+    for c in range(x[1], x[2], x[3]):
+        m |= 1 << c
+    return m
+
+
+def mask_of(es):
+    m = 0
+    for e in es:
+        m |= 1 << e
+    return m
+
+
+def route(src, dst, T, topo):
+    if topo.may_write(src, dst):
+        return dst, dst
+    c = [k for k in topo.cores_of(src) if topo.may_write(k, dst) and T.rank_of(k) is None]
+    c.sort(key=lambda k: topo.die(k) != topo.die(src))
+    return c[0], c[1]
+
+
+def ends(s, rank, T):
+    n = len(T.cores)
+    d = 1 if s % 2 == 0 else -1
+    return T.cores[rank], T.cores[(rank + d) % n]
+
+
+def land(T, s, which):
+    a = 128 + K * s
+    return T.ql[:, a:a + K].bitcast(dt.uint8) if which == 0 else T.sld[:, a:a + K]
+
+
+def halves(src, dst, topo):
+    e = topo.engines(src, dst)
+    return e[:len(e) // 2], e[len(e) // 2:]
+
+
+def arrivals(s, rank, T, topo):
+    n = len(T.cores)
+    src, dst = ends(s, (rank - (1 if s % 2 == 0 else -1)) % n, T)
+    via = route(src, dst, T, topo)
+    if via[0] == dst:
+        return len(topo.engines(src, dst))
+    return sum(len(topo.engines(k, dst)) for k in via)
+
+
+def relay_program(g, core, T, topo):
+    total = 0
+    for s in range(6):
+        for r in range(len(T.cores)):
+            src, dst = ends(s, r, T)
+            via = route(src, dst, T, topo)
+            for w in range(2):
+                if via[w] == core:
+                    g.wait_ge(T.sem["arr%d" % s], len(halves(src, core, topo)[w]))
+                    rid, pid = topo.addr(dst, core)
+                    g.remote_dma(land(T, s, w), land(T, s, w), T.sem["arr%d" % s], T.sem.snt, pid, rid, topo.mask(core, dst))
+                    total += len(topo.engines(core, dst))
+    if total:
+        g.wait_ge(T.sem.snt, total)
+
+
+def rank_program(g, core, T, topo):
+    rank = T.rank_of(core)
+    if rank is None:
+        relay_program(g, core, T, topo)
+        return
+    ops = []
+    ndma = [0]
+    sent = [0]
+
+    def ap(x):
+        if not isinstance(x, tuple):
+            return x
+        if x[0] == "*":
+            return ap(x[1]).indirect(ap(x[2]))
+        return T[x[0]][:, x[1]:x[2]] if x[3] == 1 else T[x[0]][:, x[1]:x[2]:x[3]]
+
+    def add(eng, fn, rd, wr, waits=(), dma=False):
+        r, w = [], []
+        for x in rd:
+            if isinstance(x, tuple):
+                r += [x[1], x[2]] if x[0] == "*" else [x]
+        for x in wr:
+            if x[0] == "*":
+                w.append(x[1])
+                r.append(x[2])
+            else:
+                w.append(x)
+        o = {"eng": eng, "fn": fn, "r": [(x[0], bits(x)) for x in r], "w": [(x[0], bits(x)) for x in w],
+             "waits": list(waits), "dma": None}
+        if dma:
+            o["dma"] = "d%d" % ndma[0]
+            ndma[0] += 1
+        ops.append(o)
+
+    def ts(out, in0, s1, op0, s2=None, op1=None):
+        if op1 is None:
+            add("V", lambda e: e.tensor_scalar(ap(out), ap(in0), ap(s1), None, op0), [in0, s1], [out])
+        else:
+            add("V", lambda e: e.tensor_scalar(ap(out), ap(in0), ap(s1), ap(s2), op0, op1), [in0, s1, s2], [out])
+
+    def tt(out, a, b, op):
+        add("V", lambda e: e.tensor_tensor(ap(out), ap(a), ap(b), op), [a, b], [out])
+
+    def cp(out, a):
+        add("V", lambda e: e.tensor_copy(ap(out), ap(a)), [a], [out])
+
+    def ms(out, c):
+        add("V", lambda e: e.memset(ap(out), c), [], [out])
+
+    def scan(out, d0, d1, init, op0, op1):
+        add("V", lambda e: e.tensor_tensor_scan(ap(out), ap(d0), ap(d1), init, op0, op1), [d0, d1], [out])
+
+    def act(out, a, func, bias=None, scale=None, acc=None):
+        kw = {}
+        if bias is not None:
+            kw["bias"] = ap(bias)
+        if scale is not None:
+            kw["scale"] = ap(scale)
+        if acc is not None:
+            kw["accum_out"] = ap(acc)
+        add("A", lambda e: e.activation(ap(out), ap(a), func, **kw), [a, bias, scale], [out] + ([acc] if acc else []))
+
+    def quant(q, s, a, n, src):
+        add("V", lambda e: e.quantize_mx(T[q][:, a:a + n], T[s][:, a:a + n], ap(src)), [src], [v(q, a, a + n), v(s, a, a + n)])
+
+    def mm(bank, lq, ls, la, rq, rs_, ra, n, start=True, stop=True, waits=()):
+        add("T", lambda e: e.matmul_mx(T[bank][:, 0:n], T[lq][:, la:la + 128], T[ls][:, la:la + 128],
+                                       T[rq][:, ra:ra + n], T[rs_][:, ra:ra + n], start, stop),
+            [v(lq, la, la + 128), v(ls, la, la + 128), v(rq, ra, ra + n), v(rs_, ra, ra + n)], [v(bank, 0, n)], waits)
+
+    def iota(out, pat, base, cm, flt=True):
+        if flt:
+            add("G", lambda e: e.iota(ap(out), pat, base, cm, allow_small_or_imprecise_dtypes=True), [], [out])
+        else:
+            add("G", lambda e: e.iota(ap(out), pat, base, cm), [], [out])
+
+    def diagonal(out, src, n, fill):
+        add("G", lambda e: e.affine_select(ap(out), ap(src), [[1, n]], OP.not_equal, fill, -3, -4), [src], [out])
+
+    def dma(eng, out, in_, rd, wr):
+        add(eng, lambda e: e.dma_start(out, in_), rd, wr, dma=True)
+
+    def send(s):
+        src, dst = ends(s, rank, T)
+        via = route(src, dst, T, topo)
+        for w in range(2):
+            es = halves(src, via[w], topo)[w]
+            rid, pid = topo.addr(via[w], src)
+            frm = T.qs[:, 128 * s:128 * s + K].bitcast(dt.uint8) if w == 0 else T.ss[:, 128 * s:128 * s + K]
+            sent[0] += len(es)
+            add("G", lambda e, frm=frm, w=w, rid=rid, pid=pid, es=es: e.remote_dma(
+                land(T, s, w), frm, T.sem["arr%d" % s], T.sem.snt, pid, rid, mask_of(es)),
+                [v("qs" if w == 0 else "ss", 128 * s, 128 * s + K)], [])
+
+    def col(i):
+        return v("cf", i, i + 1)
+    cR, cG, cT, cQ, cR1, cQ1, cSR, cIR, cSE, cST = [col(i) for i in range(10)]
+
+    def small(i):
+        return v("sm", 16 * i, 16 * i + 16)
+
+    def spread(out, i, n):
+        act(out, ind(small(i), v("rr", 0, n // 16)), AF.Copy)
+
+    def horner(i, jt, c0, c1, big):
+        ts(v("ktm", 16 * i, 16 * i + 16), v(jt, 0, 16), c0, OP.not_equal)
+        ts(v("ktn", 16 * i, 16 * i + 16), v(jt, 0, 16), c1, OP.is_equal, big - 1.0, OP.mult)
+
+    dma("S", T.X[:, 0:2 * C], T.x[:, 0:2 * C], [], [v("X", 0, 2 * C)])
+    dma("A", T.ub[:], T.u[:], [], [v("ub", 0, 512)])
+    dma("S", T.X[:, 2 * C:4 * C], T.x[:, 2 * C:4 * C], [], [v("X", 2 * C, 4 * C)])
+    dma("S", T.cli[:], T.cl[:], [], [v("cli", 0, 80)])
+    dma("S", T.qw[:].bitcast(dt.uint8), T.wc[:], [], [v("qw", 0, 512)])
+    dma("S", T.sw[:], T.ws[:], [], [v("sw", 0, 512)])
+    dma("S", T.vb[:], T.v[:], [], [v("vb", 0, 512)])
+
+    iota(v("pint", 0, 1), [[1, 1]], 0, 1, False)
+    iota(v("j16", 0, K), [[0, 6], [1, 16]], 0, 0)
+    iota(v("uoi", 8, 40), [[1, 8], [0, 4]], 0, 0, False)
+    iota(v("uoi", 0, 8), [[16, 8]], 0, 0, False)
+    iota(v("j4", 0, 16), [[0, 4], [1, 4]], 0, 0)
+    iota(v("cnt", 0, 22), [[-16, 22]], C - 16, 0)
+    iota(v("idt", 0, PW), [[1, PW]], 0, 0)
+    pi = v("pint", 0, 1)
+    ts(v("pint", 1, 2), pi, 15, OP.bitwise_and)
+    ts(v("pint", 2, 3), pi, 4, OP.logical_shift_right)
+    ts(v("pint", 3, 4), pi, 3, OP.bitwise_and)
+    ts(v("pint", 4, 5), pi, 2, OP.logical_shift_right, 3, OP.bitwise_and)
+    ms(v("rs", 0, 1), 0.0)
+    cp(v("cf", 0, 4), v("pint", 1, 5))
+    ts(small(1), v("j16", 0, 16), 0.0, OP.is_equal, BIG, OP.mult)
+    ts(v("rr", 0, 22), v("j16", 0, 22), 0.0, OP.mult, cR, OP.add)
+    ts(small(0), v("j16", 0, 16), cR, OP.not_equal, BIG, OP.mult)
+    ts(small(5), v("j16", 0, 16), cG, OP.is_equal)
+    cp(v("uoff", 0, 40), v("uoi", 0, 40))
+    spread(v("msel", 0, C), 0, C)
+    spread(v("mres", 0, C), 1, C)
+    act(v("ab", 0, 512), ind(small(5), v("uoff", 8, 40)), AF.Copy)
+    ts(cR1, cR, 1.0, OP.add)
+    ts(cQ1, cQ, 1.0, OP.add)
+    ts(cSR, cR, 15.0, OP.is_equal, 2.0 ** -14, OP.max)
+    ts(col(10), cR, 15.0, OP.not_equal, 2.0 ** 14, OP.mult)
+    ts(cSE, cQ, 3.0, OP.is_equal, 2.0 ** -14, OP.max)
+    ts(col(11), cR, 15.0, OP.is_equal, 2.0 ** 22, OP.mult)
+    horner(2, "j16", cR, cR1, 2.0 ** 14)
+    horner(3, "j4", cQ, cQ1, 2.0 ** 14)
+    horner(4, "j16", cR, cR1, 2.0 ** 28)
+    ts(cIR, col(10), 1.0, OP.max)
+    ts(cST, col(11), 2.0 ** -6, OP.max)
+    tt(v("sm", 32, 80), v("ktm", 32, 80), v("ktn", 32, 80), OP.add)
+    quant("qu0", "su0", 0, 128, v("ub", 0, 512))
+    add("V", lambda e: e.tensor_copy(T.qu[:].bitcast(dt.uint32), T.qu0[:].bitcast(dt.uint32).indirect(T.uoff[:, 0:8])),
+        [v("qu0", 0, 128), v("uoff", 0, 8)], [v("qu", 0, 128)])
+    add("A", lambda e: e.activation(T.su[:], T.su0[:].indirect(T.uoff[:, 0:8]), AF.Copy),
+        [v("su0", 0, 128), v("uoff", 0, 8)], [v("su", 0, 128)])
+    diagonal(v("a0b", 0, 512), v("ab", 0, 512), 512, -16384.0)
+    iota(v("zb", 0, 516), [[0, 516]], 0, 0)
+    diagonal(v("eb", 0, 516), v("zb", 0, 516), 516, 0.5)
+    spread(v("kr", 0, C), 2, C)
+    act(v("val", 0, C), v("idt", 0, C), AF.Identity, bias=cT, scale=4.0)
+    spread(v("ke", 0, K), 3, K)
+
+    def setup_gap():
+        for i in range(6):
+            lo = 16 * TILES[i][-1] if i < 5 else 0
+            ms(v("ct", 4 * (TOFF[i] + lo), 4 * (TOFF[i] + TWID[i])), 0.0)
+
+    def setup_count():
+        quant("qa", "sa", 128, 128, v("ab", 0, 512))
+        quant("qa", "sa", 0, 128, v("a0b", 0, 512))
+        ms(v("E", 4 * K, 512), 0.0)
+        ts(v("cnt", 0, 22), v("cnt", 0, 22), cR, OP.add)
+        cp(v("clu", 0, 80), v("cli", 0, 80))
+
+    def setup_rest():
+        iota(v("k1", 0, K), [[1, 6], [0, 16]], 1, 0)
+        iota(v("kw", 0, C), [[0, C]], -1, 0)
+        iota(v("f0", 0, 6 * FW), [[0, 6 * FW]], -1, 0)
+        act(v("gf", 0, 1280), ind(v("idt", 0, PW), v("clu", 0, 80)), AF.Copy)
+        spread(v("kt", 0, A), 4, A)
+        quant("ql", "sld", 0, 128, v("zb", 0, 512))
+        for b in range(4):
+            quant("qe", "se", 128 * b, 128, v("eb", 3 - b, 515 - b))
+        ms(v("cur", 0, 20), 0)
+        ms(v("mk", A, 6 * FW, FW), 4096.0)
+        ms(v("H", A, 4 * HW, HW), 0.0)
+        ms(v("V", 4 * K, 512), 0.0)
+        ms(v("cw", 20, 32), 0.0)
+        ts(v("ktm", 0, K), v("j16", 0, K), cR, OP.is_equal)
+        tt(v("ktn", 0, K), v("ktm", 0, K), v("k1", 0, K), OP.mult)
+        ts(v("kw", C, PW), v("ktn", 0, K), -1.0, OP.add)
+
+    def setup_lists():
+        for i in range(4):
+            scan(v("sl", A * i, A * i + A), v("kr", 0, A), v("gf", i, 1280, 4), 0.0, OP.mult, OP.add)
+        cp(v("kt", A, 2 * A), v("kt", 0, A))
+        ts(v("li", 0, 80), v("sl", 15, 1280, 16), cSR, OP.mult)
+        cp(v("kt", 2 * A, 4 * A), v("kt", 0, 2 * A))
+        cp(v("loff", 0, 80), v("li", 0, 80))
+        for i in range(4):
+            n = (i + 1) % 4
+            ts(v("pay", 20 * i, 20 * i + 20), v("li", 20 * n, 20 * n + 20), 512.0, OP.mult, float(i << 18), OP.add)
+        tt(v("pay", 0, 80), v("pay", 0, 80), v("li", 0, 80), OP.add)
+
+    def slot(i, t, n):
+        return v("ct", 4 * TOFF[i] + t, 4 * (TOFF[i] + n), 4)
+
+    def qtile(i):
+        quant("qc", "sc", TOFF[i], TWID[i], v("ct", 4 * TOFF[i], 4 * (TOFF[i] + TWID[i])))
+
+    def mtile(i):
+        mm("p2", "qa", "sa", 0 if i == 0 else 128, "qc", "sc", TOFF[i], TWID[i], i == 0, i == 5)
+
+    def ctile(i, joff):
+        for t, m in enumerate(TILES[i]):
+            ts(slot(i, t, 16 * m), v("p0", 0, 16 * m), v("ex", 16 * m + 15, 16 * m + 16), OP.is_ge)
+            act(v("junk", joff[0], joff[0] + 16 * m), slot(i, t, 16 * m), AF.Copy, acc=v("rs", m, m + 1))
+            joff[0] += 16 * m
+
+    for t_ in range(R):
+        sG, sB = 2 * t_, 2 * t_ + 1
+        quant("qx", "sx", 0, C, v("X", 0, 4 * C))
+        mm("p0", "qu", "su", 0, "qx", "sx", 0, C)
+        mm("p1", "qu", "su", 0, "qx", "sx", 0, C - 16)
+        if t_ == 0:
+            setup_gap()
+        tt(v("t1", 0, C), v("p0", 0, C), v("msel", 0, C), OP.add)
+        scan(v("ex", 0, C), v("mres", 0, C), v("t1", 0, C), 0.0, OP.add, OP.min)
+        for t, m in enumerate(TILES[0]):
+            act(v("sg", C * t, C * t + 16 * m), v("p1", 0, 16 * m), AF.Sign, bias=v("ex", 16 * m + 15, 16 * m + 16), scale=-1.0)
+        for t, m in enumerate(TILES[0]):
+            act(slot(0, t, 16 * m), v("sg", C * t, C * t + 16 * m), AF.Sign, bias=1.0, scale=-1.0, acc=v("rs", m, m + 1))
+        tt(slot(0, 3, C), v("p0", 0, C), v("ex", 0, C), OP.is_gt)
+        joff = [0]
+        ctile(1, joff)
+        ctile(2, joff)
+        if t_ == 0:
+            setup_count()
+        qtile(1)
+        qtile(0)
+        mtile(0)
+        mtile(1)
+        ctile(3, joff)
+        qtile(2)
+        mtile(2)
+        ctile(4, joff)
+        qtile(3)
+        mtile(3)
+        ctile(5, joff)
+        qtile(4)
+        mtile(4)
+        qtile(5)
+        mtile(5)
+        tt(v("rs1", 0, 22), v("rs", 0, 22), v("cnt", 0, 22), OP.add)
+        scan(v("cs", 0, C), v("kr", 0, C), v("p2", 0, C), 0.0, OP.mult, OP.add)
+        ts(v("rs2", 0, 22), v("rs1", 0, 22), cIR, OP.mult)
+        tt(v("ru", 0, 22), v("rs2", 0, 22), v("cs", 15, C, 16), OP.subtract)
+        ts(v("roff", 0, 22), v("ru", 0, 22), cSR, OP.mult, 0.4, OP.add)
+        cp(ind(v("win", 0, C), v("roff", 0, 22)), v("val", 0, C))
+        scan(v("es", 0, K), v("ke", 0, K), v("win", 0, K), 0.0, OP.mult, OP.add)
+        ts(v("eoff", 0, 24), v("es", 3, K, 4), cSE, OP.mult, 0.1, OP.add)
+        act(v("E", 192, 384), ind(v("X", 0, 4 * C), v("eoff", 12, 24)), AF.Copy)
+        cp(v("E", 0, 192), ind(v("X", 0, 4 * C), v("eoff", 0, 12)))
+        quant("qs", "ss", 128 * sG, 128, v("E", 0, 512))
+        send(sG)
+        if t_ == 0:
+            setup_rest()
+        for b in range(4):
+            act(v("ph", PW * b, PW * b + C), v("X", b, 4 * C, 4), AF.Copy, scale=0.5)
+        ts(v("tw", 0, C), v("p0", 0, C), 0.0, OP.is_gt, cST, OP.mult)
+        for i in range(4):
+            ts(v("wi", 20 * i, 20 * i + 20), v("cur", 0, 20), float(7 - i), OP.add)
+        ts(v("wj", 0, 80), v("wi", 0, 80), 3, OP.bitwise_and)
+        ts(v("pt", 0, 80), v("wj", 0, 80), 2.0 ** 20, OP.mult)
+        if t_ == 0:
+            setup_lists()
+        tt(v("base", 0, 80), v("pt", 0, 80), v("pay", 0, 80), OP.add)
+        if t_ == R - 1:
+            quant("qv", "sv", 0, 128, v("vb", 0, 512))
+        la = 128 + K * sG - 32
+        mm("p3", "qu", "su", 0, "ql", "sld", la, 128, waits=[("arr%d" % sG, arrivals(sG, rank, T, topo))])
+        for b in range(4):
+            mm("p%d" % (4 + b), "qe", "se", 128 * b, "ql", "sld", la, 128)
+        ts(v("tw", C, PW), v("p3", 32, 128), 0.0, OP.is_gt, cST, OP.mult)
+        cut = 34
+        act(v("tg", 16 * cut, 1280), ind(v("tw", 0, PW), v("loff", cut, 80)), AF.Copy)
+        cp(v("tg", 0, 16 * cut), ind(v("tw", 0, PW), v("loff", 0, cut)))
+        for b in range(4):
+            act(v("ph", PW * b + C, PW * b + PW), v("p%d" % (4 + b), 32, 128), AF.Copy)
+        scan(v("ts", 0, 16 * cut), v("kt", 0, 16 * cut), v("tg", 0, 16 * cut), 0.0, OP.mult, OP.add)
+        scan(v("ts", 16 * cut, 1280), v("kt", 16 * cut, 1280), v("tg", 16 * cut, 1280), 0.0, OP.mult, OP.add)
+        tt(v("key", 0, 80), v("ts", 15, 1280, 16), v("base", 0, 80), OP.add)
+        tt(v("m1", 0, 40), v("key", 0, 40), v("key", 40, 80), OP.max)
+        tt(v("mi", 0, 20), v("m1", 0, 20), v("m1", 20, 40), OP.max)
+        ts(v("oti", 0, 20), v("mi", 0, 20), 511, OP.bitwise_and)
+        ts(v("oti", 20, 40), v("mi", 0, 20), 9, OP.logical_shift_right, 511, OP.bitwise_and)
+        cp(v("ooff", 0, 40), v("oti", 0, 40))
+        cp(v("kg", 0, A), ind(v("kw", 0, PW), v("ooff", 0, 20)))
+        for h in range(2):
+            for b in range(4):
+                pl = v("ph", PW * b, PW * b + PW)
+                za = v("za", 640 * h + 160 * b, 640 * h + 160 * b + 160)
+                act(za, ind(pl, v("ooff", 10 * h, 10 * h + 10)), AF.Copy)
+                tt(v("Z", 640 * h + b, 640 * h + 640, 4), ind(pl, v("ooff", 20 + 10 * h, 30 + 10 * h)), za, OP.add)
+            quant("qz", "sz", 160 * h, 160, v("Z", 640 * h, 640 * h + 640))
+            for b in range(4):
+                mm("p%d" % ((4 + b) if h == 0 else b), "qw", "sw", 128 * b, "qz", "sz", 160 * h, 160)
+        if t_ == 0:
+            ms(v("f0", 0, 6 * FW, FW), 4096.0)
+            ms(v("f0", A, 6 * FW, FW), 160.0)
+        for c in range(6):
+            if c < 3:
+                ts(v("mk", FW * c, FW * c + A), v("kg", 0, A), float(c), OP.not_equal, 1024.0, OP.mult)
+            else:
+                act(v("mk", FW * c, FW * c + A), v("kg", 0, A), AF.Abs, bias=col(9 + c), scale=1024.0)
+        for h in range(2):
+            for b in range(4):
+                act(v("H", HW * b + 160 * h, HW * b + 160 * h + 160), v("p%d" % ((4 + b) if h == 0 else b), 0, 160),
+                    AF.Copy, scale=0.03125)
+        scan(v("fs", 0, 6 * FW), v("f0", 0, 6 * FW), v("mk", 0, 6 * FW), 0.0, OP.add, OP.min)
+        ts(v("foff", 0, 6), v("fs", A, 6 * FW, FW), 159.0, OP.add, float(A), OP.min)
+        for b in range(4):
+            src = ind(v("H", HW * b, HW * b + HW), v("foff", 0, 6))
+            if b < 2:
+                cp(v("V", b, 4 * K, 4), src)
+            else:
+                act(v("V", b, 4 * K, 4), src, AF.Copy)
+        quant("qs", "ss", 128 * sB, 128, v("V", 0, 512))
+        send(sB)
+        act(v("eh", 0, 4 * K), v("E", 0, 4 * K), AF.Copy, scale=0.5)
+        ts(v("cur", 0, 20), v("mi", 0, 20), 18, OP.logical_shift_right, 3, OP.bitwise_and)
+        if t_ == R - 1:
+            cp(v("cw", 0, 20), v("cur", 0, 20))
+            add("V", lambda e: e.transpose(T.cwt[:], T.cw[:]), [v("cw", 0, 32)], [v("cwt", 0, 32)])
+            for gg in range(8):
+                a, h = gg // 2, gg % 2
+                dma("S", T.ow[gg:gg + 1, :], T.cwt[32 * a:32 * a + 20, 16 * h:16 * h + 16], [v("cwt", 0, 32)], [])
+        la = 128 + K * sB - 32
+        for b in range(4):
+            mm("p%d" % (4 + b), "qe", "se", 128 * b, "ql", "sld", la, 128,
+               waits=[("arr%d" % sB, arrivals(sB, rank, T, topo))] if b == 0 else [])
+        for b in range(4):
+            tt(v("upd", b, 4 * K, 4), v("p%d" % (4 + b), 32, 128), v("eh", b, 4 * K, 4), OP.add)
+        cp(ind(v("X", 0, 4 * C), v("eoff", 0, 24)), v("upd", 0, 4 * K))
+
+    quant("qx", "sx", 0, C, v("X", 0, 4 * C))
+    mm("p0", "qv", "sv", 0, "qx", "sx", 0, C)
+    dma("S", T.oc[:], T.qx[:].bitcast(dt.uint8), [v("qx", 0, C)], [])
+    for k in range(4):
+        dma("A", T.osc[4 * k:4 * k + 4, :], T.sx[32 * k:32 * k + 4, :], [v("sx", 0, C)], [])
+    cp(v("yb", 0, C), v("p0", 0, C))
+    dma("S", T.y[:], T.yb[:], [v("yb", 0, C)], [])
+
+    tail = ops[:]
+    del ops[:]
+    for c in range(3, 6):
+        ms(col(9 + c), -1024.0 * c)
+    ops.extend(tail)
+    emit(g, T, ops, sent[0])
+
+
+def emit(g, T, ops, sent):
+    q = {"V": g.vector, "A": g.scalar, "T": g.tensor, "G": g, "S": g.sync}
+    known = {e: {} for e in q}
+    hist = {}
+    need = set()
+    for i, o in enumerate(ops):
+        deps = set()
+        for kind in ("r", "w"):
+            for name, m in o[kind]:
+                bank = SCRATCH[name][0] == "psum"
+                for (j, jm, jw) in hist.get(name, []):
+                    same = ops[j]["eng"] == o["eng"] and ops[j]["dma"] is None and o["dma"] is None
+                    if bank:
+                        if not same:
+                            deps.add(j)
+                    elif (jm & m) and (jw or kind == "w"):
+                        deps.add(j)
+        kn = known[o["eng"]]
+        o["deps"] = []
+        for j in sorted(deps, reverse=True):
+            src = ops[j]["dma"] or ops[j]["eng"]
+            if kn.get(src, -1) >= j:
+                continue
+            o["deps"].append(j)
+            need.add(j)
+            kn[src] = j
+            for s, k in ops[j]["clock"].items():
+                if kn.get(s, -1) < k:
+                    kn[s] = k
+        o["clock"] = dict(kn)
+        for name, m in o["w"]:
+            h = [x for x in hist.get(name, []) if x[1] & ~m or SCRATCH[name][0] == "psum"]
+            hist[name] = h + [(i, m, True)]
+        for name, m in o["r"]:
+            hist.setdefault(name, []).append((i, m, False))
+    count = {e: 0 for e in q}
+    waited = set()
+    for i, o in enumerate(ops):
+        e = q[o["eng"]]
+        for s, n in o["waits"]:
+            e.wait_ge(T.sem[s], n)
+        for j in o["deps"]:
+            if ops[j]["dma"]:
+                e.wait_ge(T.sem[ops[j]["dma"]], 16)
+                waited.add(j)
+            else:
+                e.wait_ge(T.sem["e" + ops[j]["eng"]], ops[j]["at"])
+        ins = o["fn"](e)
+        if o["dma"]:
+            ins.then_inc(T.sem[o["dma"]], 16)
+        elif i in need:
+            count[o["eng"]] += 1
+            o["at"] = count[o["eng"]]
+            ins.then_inc(T.sem["e" + o["eng"]], 1)
+    for i, o in enumerate(ops):
+        if o["dma"] and i not in waited:
+            q[o["eng"]].wait_ge(T.sem[o["dma"]], 16)
+    g.wait_ge(T.sem.snt, sent)

@@ -1,3 +1,4 @@
+from concourse.bass import DstId, RemoteDMATransfer
 from concourse.mybir import dt, AluOpType, ActivationFunctionType
 
 C, K, A, R = 352, 96, 320, 3
@@ -9,6 +10,9 @@ TILES = [[21, 20, 19], [18, 17, 16, 15], [14, 13, 12, 11], [10, 9, 8, 7], [6, 5,
 TWID = [352, 288, 224, 160, 128, 128]
 TOFF = [sum(TWID[:i]) for i in range(6)]
 X4, U8 = "float8_e4m3fn_x4", "uint8"
+LO = 192
+PAR = {"nb": 5, "e": (5, 6, 7, 8, 9, 10), "cut": [30, 68], "zh": 160, "ma": 3, "kgA": False,
+       "qord": [(2, 3), (0, 3), (3, 4), (1, 4), (4, 5), (5, 5)]}
 
 
 def _sb(n, d):
@@ -16,38 +20,40 @@ def _sb(n, d):
 
 
 SCRATCH = {
-    "X": _sb(4 * C, "bfloat16"), "qx": _sb(C, X4), "sx": _sb(C, U8),
+    "Xa": _sb(4 * PW, "bfloat16"), "Xb": _sb(4 * PW, "bfloat16"), "qx": _sb(C, X4), "sx": _sb(C, U8),
     "ub": _sb(512, "bfloat16"), "qu0": _sb(128, X4), "su0": _sb(128, U8), "qu": _sb(128, X4), "su": _sb(128, U8),
     "vb": _sb(512, "bfloat16"), "qv": _sb(128, X4), "sv": _sb(128, U8),
     "qw": _sb(512, X4), "sw": _sb(512, U8),
     "cli": _sb(80, "int32"), "clu": _sb(80, "uint16"),
-    "pint": _sb(8, "int32"), "cf": _sb(16, "float32"), "uoi": _sb(40, "int32"), "uoff": _sb(40, "uint16"),
+    "pint": _sb(8, "int32"), "cf": _sb(20, "float32"), "uoi": _sb(40, "int32"), "uoff": _sb(40, "uint16"),
     "idt": _sb(PW, "float32"), "j16": _sb(K, "float32"), "j4": _sb(16, "float32"), "k1": _sb(K, "float32"),
     "sm": _sb(96, "float32"), "rr": _sb(22, "uint16"), "eb": _sb(516, "bfloat16"),
     "ab": _sb(512, "bfloat16"), "a0b": _sb(512, "bfloat16"), "zb": _sb(516, "bfloat16"),
     "qa": _sb(256, X4), "sa": _sb(256, U8), "qe": _sb(512, X4), "se": _sb(512, U8),
     "msel": _sb(C, "float32"), "mres": _sb(C, "float32"), "kr": _sb(C, "float32"), "ktm": _sb(K, "float32"),
-    "ktn": _sb(K, "float32"), "kt": _sb(1280, "bfloat16"), "ke": _sb(K, "float32"), "val": _sb(C, "float32"),
+    "ktn": _sb(K, "float32"), "kt": _sb(1280, "bfloat16"), "ke": _sb(C, "float32"), "val": _sb(C, "float32"),
+    "tab": _sb(C, "float32"), "iv": _sb(C, "float32"), "ivs": _sb(C, "float32"), "xoff": _sb(88, "uint16"),
     "cnt": _sb(22, "float32"), "kw": _sb(PW, "bfloat16"), "f0": _sb(6 * FW, "bfloat16"),
     "gf": _sb(1280, "float32"), "sl": _sb(1280, "float32"), "li": _sb(80, "int32"), "loff": _sb(80, "uint16"),
     "pay": _sb(80, "float32"), "pt": _sb(80, "float32"), "cur": _sb(20, "int32"), "wi": _sb(80, "int32"),
-    "wj": _sb(80, "int32"), "base": _sb(80, "float32"),
+    "wj": _sb(80, "int32"), "base": _sb(80, "float32"), "kd": _sb(80, "float32"),
     "t1": _sb(C, "float32"), "ex": _sb(C, "float32"), "ct": _sb(4 * 1280, "bfloat16"),
-    "qc": _sb(1280, X4), "sc": _sb(1280, U8), "sg": _sb(3 * C, "bfloat16"), "junk": _sb(2752, "bfloat16"),
+    "qc": _sb(1280, X4), "sc": _sb(1280, U8), "sg": _sb(2400, "bfloat16"), "junk": _sb(3072 + 16 * 256, "bfloat16"),
+    "one": _sb(256, "bfloat16"),
     "rs": _sb(22, "float32"), "rs1": _sb(22, "float32"), "rs2": _sb(22, "float32"), "cs": _sb(C, "float32"),
     "ru": _sb(22, "float32"), "roff": _sb(22, "uint16"), "win": _sb(C, "float32"), "es": _sb(K, "float32"),
     "eoff": _sb(24, "uint16"), "E": _sb(512, "bfloat16"), "eh": _sb(4 * K, "bfloat16"),
     "qs": _sb(6 * 128, X4), "ss": _sb(6 * 128, U8), "ql": _sb(128 + 6 * K, X4), "sld": _sb(128 + 6 * K, U8),
     "ph": _sb(4 * PW, "bfloat16"), "tw": _sb(PW, "bfloat16"), "tg": _sb(1280, "bfloat16"), "ts": _sb(1280, "bfloat16"),
-    "key": _sb(80, "float32"), "m1": _sb(40, "float32"), "mi": _sb(20, "int32"), "oti": _sb(40, "int32"),
+    "key": _sb(80, "float32"), "mi": _sb(20, "int32"), "oti": _sb(40, "int32"),
     "ooff": _sb(40, "uint16"), "za": _sb(1280, "bfloat16"), "Z": _sb(1280, "bfloat16"), "qz": _sb(A, X4), "sz": _sb(A, U8),
-    "H": _sb(4 * HW, "bfloat16"), "kg": _sb(A, "bfloat16"), "mk": _sb(6 * FW, "bfloat16"), "fs": _sb(6 * FW, "bfloat16"),
-    "foff": _sb(6, "uint16"), "V": _sb(512, "bfloat16"), "upd": _sb(4 * K, "bfloat16"),
+    "H": _sb(4 * HW, "bfloat16"), "mk": _sb(6 * FW, "bfloat16"), "fs": _sb(6 * FW, "bfloat16"),
+    "foff": _sb(6, "uint16"), "V": _sb(512, "bfloat16"),
     "cw": _sb(32, "float32"), "cwt": _sb(32, "float32"), "yb": _sb(C, "float32"),
 }
 for _b in range(8):
     SCRATCH["p%d" % _b] = ("psum", [128, 512], "float32")
-NDMA = 24
+NDMA = 28
 SEMAPHORES = (["eV", "eA", "eT", "eG", "snt"] + ["arr%d" % _s for _s in range(6)] + ["d%d" % _s for _s in range(NDMA)])
 
 OP, AF = AluOpType, ActivationFunctionType
@@ -77,37 +83,31 @@ def mask_of(es):
     return m
 
 
-def route(src, dst, T, topo):
-    if topo.may_write(src, dst):
-        return dst, dst
-    c = [k for k in topo.cores_of(src) if topo.may_write(k, dst) and T.rank_of(k) is None]
-    c.sort(key=lambda k: topo.die(k) != topo.die(src))
-    return c[0], c[1]
-
-
 def ends(s, rank, T):
     n = len(T.cores)
     d = 1 if s % 2 == 0 else -1
     return T.cores[rank], T.cores[(rank + d) % n]
 
 
-def land(T, s, which):
-    a = 128 + K * s
-    return T.ql[:, a:a + K].bitcast(dt.uint8) if which == 0 else T.sld[:, a:a + K]
+def pieces(src, dst, T, topo):
+    if topo.may_write(src, dst):
+        a = b = dst
+    else:
+        c = [k for k in topo.cores_of(src) if topo.may_write(k, dst) and T.rank_of(k) is None]
+        a = [k for k in c if topo.die(k) == topo.die(src)][0]
+        b = [k for k in c if topo.die(k) != topo.die(src)][0]
+    return [[(a, 0, 0, K, topo.engines(src, a))], [(b, 1, 0, K, topo.engines(src, b))]]
 
 
-def halves(src, dst, topo):
-    e = topo.engines(src, dst)
-    return e[:len(e) // 2], e[len(e) // 2:]
+def land(T, s, which, a, b):
+    o = 128 + K * s
+    return T.ql[:, o + a:o + b].bitcast(dt.uint8) if which == 0 else T.sld[:, o + a:o + b]
 
 
 def arrivals(s, rank, T, topo):
     n = len(T.cores)
     src, dst = ends(s, (rank - (1 if s % 2 == 0 else -1)) % n, T)
-    via = route(src, dst, T, topo)
-    if via[0] == dst:
-        return len(topo.engines(src, dst))
-    return sum(len(topo.engines(k, dst)) for k in via)
+    return sum(len(p[4]) if p[0] == dst else len(topo.engines(p[0], dst)) for call in pieces(src, dst, T, topo) for p in call)
 
 
 def relay_program(g, core, T, topo):
@@ -115,13 +115,14 @@ def relay_program(g, core, T, topo):
     for s in range(6):
         for r in range(len(T.cores)):
             src, dst = ends(s, r, T)
-            via = route(src, dst, T, topo)
-            for w in range(2):
-                if via[w] == core:
-                    g.wait_ge(T.sem["arr%d" % s], len(halves(src, core, topo)[w]))
-                    rid, pid = topo.addr(dst, core)
-                    g.remote_dma(land(T, s, w), land(T, s, w), T.sem["arr%d" % s], T.sem.snt, pid, rid, topo.mask(core, dst))
-                    total += len(topo.engines(core, dst))
+            for call in pieces(src, dst, T, topo):
+                for (via, w, a, b, es) in call:
+                    if via == core:
+                        g.wait_ge(T.sem["arr%d" % s], len(es))
+                        rid, pid = topo.addr(dst, core)
+                        g.remote_dma(land(T, s, w, a, b), land(T, s, w, a, b), T.sem["arr%d" % s], T.sem.snt, pid, rid,
+                                     topo.mask(core, dst))
+                        total += len(topo.engines(core, dst))
     if total:
         g.wait_ge(T.sem.snt, total)
 
@@ -188,6 +189,14 @@ def rank_program(g, core, T, topo):
             kw["accum_out"] = ap(acc)
         add("A", lambda e: e.activation(ap(out), ap(a), func, **kw), [a, bias, scale], [out] + ([acc] if acc else []))
 
+    def move(eng, out, a, scale=None):
+        if eng == "A":
+            act(out, a, AF.Copy, scale=scale)
+        elif scale is None:
+            cp(out, a)
+        else:
+            ts(out, a, scale, OP.mult)
+
     def quant(q, s, a, n, src):
         add("V", lambda e: e.quantize_mx(T[q][:, a:a + n], T[s][:, a:a + n], ap(src)), [src], [v(q, a, a + n), v(s, a, a + n)])
 
@@ -202,27 +211,38 @@ def rank_program(g, core, T, topo):
         else:
             add("G", lambda e: e.iota(ap(out), pat, base, cm), [], [out])
 
-    def diagonal(out, src, n, fill):
-        add("G", lambda e: e.affine_select(ap(out), ap(src), [[1, n]], OP.not_equal, fill, -3, -4), [src], [out])
+    def fill(out, c):
+        iota(out, [[0, len(range(*out[1:]))]], c, 0)
+
+    def diagonal(out, src, n, fill_):
+        add("G", lambda e: e.affine_select(ap(out), ap(src), [[1, n]], OP.not_equal, fill_, -3, -4), [src], [out])
 
     def dma(eng, out, in_, rd, wr):
         add(eng, lambda e: e.dma_start(out, in_), rd, wr, dma=True)
 
     def send(s):
         src, dst = ends(s, rank, T)
-        via = route(src, dst, T, topo)
-        for w in range(2):
-            es = halves(src, via[w], topo)[w]
-            rid, pid = topo.addr(via[w], src)
-            frm = T.qs[:, 128 * s:128 * s + K].bitcast(dt.uint8) if w == 0 else T.ss[:, 128 * s:128 * s + K]
-            sent[0] += len(es)
-            add("G", lambda e, frm=frm, w=w, rid=rid, pid=pid, es=es: e.remote_dma(
-                land(T, s, w), frm, T.sem["arr%d" % s], T.sem.snt, pid, rid, mask_of(es)),
-                [v("qs" if w == 0 else "ss", 128 * s, 128 * s + K)], [])
+        for call in pieces(src, dst, T, topo):
+            tr, rd = [], []
+            for (via, w, a, b, es) in call:
+                o = 128 * s
+                frm = T.qs[:, o + a:o + b].bitcast(dt.uint8) if w == 0 else T.ss[:, o + a:o + b]
+                sent[0] += len(es)
+                tr.append((land(T, s, w, a, b), frm, topo.addr(via, src), mask_of(es)))
+                rd.append(v("qs" if w == 0 else "ss", o + a, o + b))
+            if len(tr) == 1:
+                to, frm, (rid, pid), m = tr[0]
+                add("G", lambda e, to=to, frm=frm, rid=rid, pid=pid, m=m: e.remote_dma(
+                    to, frm, T.sem["arr%d" % s], T.sem.snt, pid, rid, m), rd, [])
+            else:
+                add("G", lambda e, tr=tr: e.remote_dma_fused(
+                    [RemoteDMATransfer(dst_ids=[DstId(rid=rid, pnc=pid)], dma_engine_mask=m, remote_sem=T.sem["arr%d" % s],
+                                       src=frm, dst=to) for (to, frm, (rid, pid), m) in tr], local_sem=T.sem.snt), rd, [])
 
     def col(i):
         return v("cf", i, i + 1)
-    cR, cG, cT, cQ, cR1, cQ1, cSR, cIR, cSE, cST = [col(i) for i in range(10)]
+    cR, cG, cT, cQ, cR1, cQ1, cSR, cIR, cSE, cST, cA, cB, cT1, cK = [col(i) for i in range(14)]
+    cNI = col(19)
 
     def small(i):
         return v("sm", 16 * i, 16 * i + 16)
@@ -234,175 +254,223 @@ def rank_program(g, core, T, topo):
         ts(v("ktm", 16 * i, 16 * i + 16), v(jt, 0, 16), c0, OP.not_equal)
         ts(v("ktn", 16 * i, 16 * i + 16), v(jt, 0, 16), c1, OP.is_equal, big - 1.0, OP.mult)
 
-    dma("S", T.X[:, 0:2 * C], T.x[:, 0:2 * C], [], [v("X", 0, 2 * C)])
+    def pad(i):
+        lo = 16 * TILES[i][-1] if i < 5 else 0
+        fill(v("ct", 4 * (TOFF[i] + lo), 4 * (TOFF[i] + TWID[i])), 0)
+
+    dma("S", T.Xa[:, 4 * LO:4 * C], T.x[:, 4 * LO:4 * C], [], [v("Xa", 4 * LO, 4 * C)])
     dma("A", T.ub[:], T.u[:], [], [v("ub", 0, 512)])
-    dma("S", T.X[:, 2 * C:4 * C], T.x[:, 2 * C:4 * C], [], [v("X", 2 * C, 4 * C)])
+    dma("S", T.Xa[:, 0:4 * LO], T.x[:, 0:4 * LO], [], [v("Xa", 0, 4 * LO)])
     dma("S", T.cli[:], T.cl[:], [], [v("cli", 0, 80)])
     dma("S", T.qw[:].bitcast(dt.uint8), T.wc[:], [], [v("qw", 0, 512)])
     dma("S", T.sw[:], T.ws[:], [], [v("sw", 0, 512)])
     dma("S", T.vb[:], T.v[:], [], [v("vb", 0, 512)])
 
     iota(v("pint", 0, 1), [[1, 1]], 0, 1, False)
-    iota(v("j16", 0, K), [[0, 6], [1, 16]], 0, 0)
+    iota(v("j16", 0, 32), [[0, 2], [1, 16]], 0, 0)
     iota(v("uoi", 8, 40), [[1, 8], [0, 4]], 0, 0, False)
     iota(v("uoi", 0, 8), [[16, 8]], 0, 0, False)
     iota(v("j4", 0, 16), [[0, 4], [1, 4]], 0, 0)
-    iota(v("cnt", 0, 22), [[-16, 22]], C - 16, 0)
-    iota(v("idt", 0, PW), [[1, PW]], 0, 0)
+    iota(v("cnt", 0, 22), [[16, 22]], 0, 0)
+    fill(v("rs2", 0, 1), 0)
+    pad(0)
     pi = v("pint", 0, 1)
     ts(v("pint", 1, 2), pi, 15, OP.bitwise_and)
     ts(v("pint", 2, 3), pi, 4, OP.logical_shift_right)
     ts(v("pint", 3, 4), pi, 3, OP.bitwise_and)
     ts(v("pint", 4, 5), pi, 2, OP.logical_shift_right, 3, OP.bitwise_and)
-    ms(v("rs", 0, 1), 0.0)
     cp(v("cf", 0, 4), v("pint", 1, 5))
-    ts(small(1), v("j16", 0, 16), 0.0, OP.is_equal, BIG, OP.mult)
+    cp(v("uoff", 0, 40), v("uoi", 0, 40))
+    ts(small(5), v("j16", 0, 16), cG, OP.is_equal)
     ts(v("rr", 0, 22), v("j16", 0, 22), 0.0, OP.mult, cR, OP.add)
     ts(small(0), v("j16", 0, 16), cR, OP.not_equal, BIG, OP.mult)
-    ts(small(5), v("j16", 0, 16), cG, OP.is_equal)
-    cp(v("uoff", 0, 40), v("uoi", 0, 40))
-    spread(v("msel", 0, C), 0, C)
-    spread(v("mres", 0, C), 1, C)
+    ms(v("mres", 0, C), 0.0)
     act(v("ab", 0, 512), ind(small(5), v("uoff", 8, 40)), AF.Copy)
+    spread(v("msel", 0, C), 0, C)
+    diagonal(v("a0b", 0, 512), v("ab", 0, 512), 512, -16384.0)
     ts(cR1, cR, 1.0, OP.add)
     ts(cQ1, cQ, 1.0, OP.add)
     ts(cSR, cR, 15.0, OP.is_equal, 2.0 ** -14, OP.max)
-    ts(col(10), cR, 15.0, OP.not_equal, 2.0 ** 14, OP.mult)
-    ts(cSE, cQ, 3.0, OP.is_equal, 2.0 ** -14, OP.max)
-    ts(col(11), cR, 15.0, OP.is_equal, 2.0 ** 22, OP.mult)
+    ts(cA, cR, 15.0, OP.not_equal, 2.0 ** 14, OP.mult)
     horner(2, "j16", cR, cR1, 2.0 ** 14)
     horner(3, "j4", cQ, cQ1, 2.0 ** 14)
-    horner(4, "j16", cR, cR1, 2.0 ** 28)
-    ts(cIR, col(10), 1.0, OP.max)
-    ts(cST, col(11), 2.0 ** -6, OP.max)
-    tt(v("sm", 32, 80), v("ktm", 32, 80), v("ktn", 32, 80), OP.add)
+    ts(cSE, cQ, 3.0, OP.is_equal, 2.0 ** -14, OP.max)
+    ts(cIR, cA, 1.0, OP.max)
+    ts(cT1, cT, 0.1, OP.add)
+    tt(v("sm", 32, 64), v("ktm", 32, 64), v("ktn", 32, 64), OP.add)
+    ts(cK, cR, C - 16 + 0.4, OP.add)
+    ts(cNI, cIR, -1.0, OP.mult)
+    ms(v("mres", 0, C, 16), BIG)
+    quant("qa", "sa", 128, 128, v("ab", 0, 512))
     quant("qu0", "su0", 0, 128, v("ub", 0, 512))
-    add("V", lambda e: e.tensor_copy(T.qu[:].bitcast(dt.uint32), T.qu0[:].bitcast(dt.uint32).indirect(T.uoff[:, 0:8])),
-        [v("qu0", 0, 128), v("uoff", 0, 8)], [v("qu", 0, 128)])
     add("A", lambda e: e.activation(T.su[:], T.su0[:].indirect(T.uoff[:, 0:8]), AF.Copy),
         [v("su0", 0, 128), v("uoff", 0, 8)], [v("su", 0, 128)])
-    diagonal(v("a0b", 0, 512), v("ab", 0, 512), 512, -16384.0)
-    iota(v("zb", 0, 516), [[0, 516]], 0, 0)
-    diagonal(v("eb", 0, 516), v("zb", 0, 516), 516, 0.5)
+    add("V", lambda e: e.tensor_copy(T.qu[:].bitcast(dt.uint32), T.qu0[:].bitcast(dt.uint32).indirect(T.uoff[:, 0:8])),
+        [v("qu0", 0, 128), v("uoff", 0, 8)], [v("qu", 0, 128)])
     spread(v("kr", 0, C), 2, C)
-    act(v("val", 0, C), v("idt", 0, C), AF.Identity, bias=cT, scale=4.0)
-    spread(v("ke", 0, K), 3, K)
-
-    def setup_gap():
-        for i in range(6):
-            lo = 16 * TILES[i][-1] if i < 5 else 0
-            ms(v("ct", 4 * (TOFF[i] + lo), 4 * (TOFF[i] + TWID[i])), 0.0)
-
-    def setup_count():
-        quant("qa", "sa", 128, 128, v("ab", 0, 512))
-        quant("qa", "sa", 0, 128, v("a0b", 0, 512))
-        ms(v("E", 4 * K, 512), 0.0)
-        ts(v("cnt", 0, 22), v("cnt", 0, 22), cR, OP.add)
-        cp(v("clu", 0, 80), v("cli", 0, 80))
+    for i in range(1, 6):
+        pad(i)
+    if PAR["e"]:
+        fill(v("one", 0, 16 * max(PAR["e"])), 1)
+    iota(v("idt", 0, PW), [[1, PW]], 0, 0)
+    iota(v("val", 0, C), [[4, C]], 0, 0)
+    fill(v("E", 4 * K, 512), 0)
+    fill(v("zb", 0, 516), 0)
+    diagonal(v("eb", 0, 516), v("zb", 0, 516), 516, 0.5)
 
     def setup_rest():
-        iota(v("k1", 0, K), [[1, 6], [0, 16]], 1, 0)
-        iota(v("kw", 0, C), [[0, C]], -1, 0)
-        iota(v("f0", 0, 6 * FW), [[0, 6 * FW]], -1, 0)
-        act(v("gf", 0, 1280), ind(v("idt", 0, PW), v("clu", 0, 80)), AF.Copy)
+        iota(v("wj", 0, 80), [[0, 20], [-1, 4]], 3, 0, False)
+        iota(v("j16", 32, K), [[0, 4], [1, 16]], 0, 0)
+        iota(v("k1", 0, K), [[1024, 6], [0, 16]], -8192, 0)
+        fill(v("kw", 0, C), 8192)
+        iota(v("cf", 14, 19), [[-1024, 5]], -1024, 0)
+        fill(v("mk", A, 6 * FW, FW), 4096)
+        fill(v("H", A, 4 * HW, HW), 0)
+        fill(v("V", 4 * K, 512), 0)
+        fill(v("f0", 0, 6 * FW), -1)
+        fill(v("f0", 0, 6 * FW, FW), 4096)
+        fill(v("f0", A, 6 * FW, FW), 160)
+        iota(v("tab", 0, K), [[4, K]], 4 * C, 0)
+        fill(v("tab", K, C), 0)
+        fill(v("cw", 20, 32), 0)
+        act(v("gf", 640, 1280), ind(v("idt", 0, PW), v("clu", 40, 80)), AF.Copy)
+        horner(4, "j16", cR, cR1, 2.0 ** 28)
+        ts(cB, cR, 15.0, OP.is_equal, 2.0 ** 22, OP.mult)
+        tt(small(4), v("ktm", 64, 80), v("ktn", 64, 80), OP.add)
+        ts(cST, cB, 2.0 ** -6, OP.max)
         spread(v("kt", 0, A), 4, A)
+        act(v("kt", A, 2 * A), v("kt", 0, A), AF.Copy)
+        act(v("kt", 2 * A, 4 * A), v("kt", 0, 2 * A), AF.Copy)
         quant("ql", "sld", 0, 128, v("zb", 0, 512))
         for b in range(4):
             quant("qe", "se", 128 * b, 128, v("eb", 3 - b, 515 - b))
-        ms(v("cur", 0, 20), 0)
-        ms(v("mk", A, 6 * FW, FW), 4096.0)
-        ms(v("H", A, 4 * HW, HW), 0.0)
-        ms(v("V", 4 * K, 512), 0.0)
-        ms(v("cw", 20, 32), 0.0)
-        ts(v("ktm", 0, K), v("j16", 0, K), cR, OP.is_equal)
-        tt(v("ktn", 0, K), v("ktm", 0, K), v("k1", 0, K), OP.mult)
-        ts(v("kw", C, PW), v("ktn", 0, K), -1.0, OP.add)
 
     def setup_lists():
         for i in range(4):
             scan(v("sl", A * i, A * i + A), v("kr", 0, A), v("gf", i, 1280, 4), 0.0, OP.mult, OP.add)
-        cp(v("kt", A, 2 * A), v("kt", 0, A))
-        ts(v("li", 0, 80), v("sl", 15, 1280, 16), cSR, OP.mult)
-        cp(v("kt", 2 * A, 4 * A), v("kt", 0, 2 * A))
-        cp(v("loff", 0, 80), v("li", 0, 80))
+        ts(v("ktm", 0, K), v("j16", 0, K), cR, OP.is_equal)
         for i in range(4):
-            n = (i + 1) % 4
-            ts(v("pay", 20 * i, 20 * i + 20), v("li", 20 * n, 20 * n + 20), 512.0, OP.mult, float(i << 18), OP.add)
+            ts(v("li", i, 80, 4), v("sl", A * i + 15, A * i + A, 16), cSR, OP.mult)
+        tt(v("ktn", 0, K), v("ktm", 0, K), v("k1", 0, K), OP.mult)
+        cp(v("loff", 0, 80), v("li", 0, 80))
+        ts(v("kw", C, PW), v("ktn", 0, K), 8192.0, OP.add)
+        for i in range(4):
+            ts(v("pay", i, 80, 4), v("li", (i + 1) % 4, 80, 4), 512.0, OP.mult, float(i << 18), OP.add)
         tt(v("pay", 0, 80), v("pay", 0, 80), v("li", 0, 80), OP.add)
 
-    def slot(i, t, n):
-        return v("ct", 4 * TOFF[i] + t, 4 * (TOFF[i] + n), 4)
+    def slot(i, t, a, b):
+        return v("ct", 4 * (TOFF[i] + a) + t, 4 * (TOFF[i] + b), 4)
+
+    WHERE = {m: (i, t) for i in range(6) for t, m in enumerate(TILES[i])}
+    BOTH = list(range(21, 21 - PAR["nb"], -1))
+    SCAN = list(PAR["e"])
+
+    def pivot(m):
+        return v("ex", 16 * m + 15, 16 * m + 16)
 
     def qtile(i):
         quant("qc", "sc", TOFF[i], TWID[i], v("ct", 4 * TOFF[i], 4 * (TOFF[i] + TWID[i])))
 
-    def mtile(i):
-        mm("p2", "qa", "sa", 0 if i == 0 else 128, "qc", "sc", TOFF[i], TWID[i], i == 0, i == 5)
+    def compare(m):
+        ts(slot(*WHERE[m], 0, 16 * m), v("p0", 0, 16 * m), pivot(m), OP.is_ge)
 
-    def ctile(i, joff):
-        for t, m in enumerate(TILES[i]):
-            ts(slot(i, t, 16 * m), v("p0", 0, 16 * m), v("ex", 16 * m + 15, 16 * m + 16), OP.is_ge)
-            act(v("junk", joff[0], joff[0] + 16 * m), slot(i, t, 16 * m), AF.Copy, acc=v("rs", m, m + 1))
-            joff[0] += 16 * m
+    def rowsum(m):
+        e_ = 3072 + 256 * (m - min(SCAN)) + 256
+        scan(v("junk", e_ - 16 * m, e_), v("one", 0, 16 * m), slot(*WHERE[m], 0, 16 * m), -16.0 * m, OP.mult, OP.add)
+
+    def order(X, first):
+        quant("qx", "sx", LO, C - LO, v(X, 4 * LO, 4 * C))
+        mm("p3", "qu", "su", 0, "qx", "sx", LO, C - LO)
+        quant("qx", "sx", 0, LO, v(X, 0, 4 * LO))
+        mm("p1", "qu", "su", 0, "qx", "sx", 0, C - 16)
+        mm("p0", "qu", "su", 0, "qx", "sx", 0, C)
+        tt(v("t1", LO, C), v("p3", 0, C - LO), v("msel", LO, C), OP.add)
+        scan(v("ex", LO, C), v("mres", LO, C), v("t1", LO, C), 0.0, OP.add, OP.min)
+        if first:
+            quant("qa", "sa", 0, 128, v("a0b", 0, 512))
+            cp(v("clu", 0, 80), v("cli", 0, 80))
+        tt(slot(0, 3, LO, C), v("p3", 0, C - LO), v("ex", LO, C), OP.is_gt)
+        tt(v("t1", 0, LO), v("p0", 0, LO), v("msel", 0, LO), OP.add)
+        lead = [m for m in range(21, LO // 16 - 1, -1) if m not in BOTH][0]
+        compare(lead)
+        scan(v("ex", 0, LO), v("mres", 0, LO), v("t1", 0, LO), 0.0, OP.add, OP.min)
+        so = 0
+        for k in range(0, len(BOTH), 2):
+            pair = [(m, so + sum(16 * n for n in BOTH[k:k + 2] if n > m)) for m in BOTH[k:k + 2]]
+            for m, o in pair:
+                act(v("sg", o, o + 16 * m), v("p1", 0, 16 * m), AF.Sign, bias=pivot(m), scale=-1.0)
+            for m, o in pair:
+                act(slot(*WHERE[m], 0, 16 * m), v("sg", o, o + 16 * m), AF.Sign, bias=1.0, scale=-1.0, acc=v("rs", m, m + 1))
+            so += sum(16 * n for n in BOTH[k:k + 2])
+        done, jo, ready, summed = [], 0, [], []
+        for i in range(6):
+            for m in TILES[i]:
+                if m in BOTH:
+                    continue
+                s_ = slot(*WHERE[m], 0, 16 * m)
+                if m != lead:
+                    compare(m)
+                if not done and m != lead:
+                    done.append(m)
+                    tt(slot(0, 3, 0, LO), v("p0", 0, LO), v("ex", 0, LO), OP.is_gt)
+                if m not in SCAN:
+                    act(v("junk", jo, jo + 16 * m), s_, AF.Identity, bias=cNI, scale=cIR, acc=v("rs2", m, m + 1))
+                    jo += 16 * m
+            for m in TILES[i]:
+                if m in SCAN and i < 5:
+                    rowsum(m)
+            for (q, after) in PAR["qord"]:
+                if after == i:
+                    qtile(q)
+                    ready.append(q)
+                    while 0 in ready + summed and ready:
+                        n = 0 if 0 in ready else ready[0]
+                        ready.remove(n)
+                        summed.append(n)
+                        mm("p2", "qa", "sa", 0 if n == 0 else 128, "qc", "sc", TOFF[n], TWID[n], n == 0, len(summed) == 6)
+        lo = min(BOTH)
+        tt(v("rs1", lo, 22), v("rs", lo, 22), v("cnt", lo, 22), OP.subtract)
+        for m in TILES[5]:
+            if m in SCAN:
+                rowsum(m)
+        ts(v("rs2", lo, 22), v("rs1", lo, 22), cIR, OP.mult)
+        if SCAN:
+            a_, b_ = min(SCAN), max(SCAN) + 1
+            ts(v("rs2", a_, b_), v("junk", 3072 + 255, 3072 + 256 * (b_ - a_), 256), cIR, OP.mult)
+        scan(v("cs", 0, C), v("kr", 0, C), v("p2", 0, C), 0.0, OP.mult, OP.add)
+        tt(v("ru", 0, 22), v("rs2", 0, 22), v("cs", 15, C, 16), OP.subtract)
+        ts(v("roff", 0, 22), v("ru", 0, 22), cSR, OP.mult, cK, OP.add)
 
     for t_ in range(R):
         sG, sB = 2 * t_, 2 * t_ + 1
-        quant("qx", "sx", 0, C, v("X", 0, 4 * C))
-        mm("p0", "qu", "su", 0, "qx", "sx", 0, C)
-        mm("p1", "qu", "su", 0, "qx", "sx", 0, C - 16)
+        X, Xn = ("Xa", "Xb") if t_ % 2 == 0 else ("Xb", "Xa")
+        order(X, t_ == 0)
         if t_ == 0:
-            setup_gap()
-        tt(v("t1", 0, C), v("p0", 0, C), v("msel", 0, C), OP.add)
-        scan(v("ex", 0, C), v("mres", 0, C), v("t1", 0, C), 0.0, OP.add, OP.min)
-        for t, m in enumerate(TILES[0]):
-            act(v("sg", C * t, C * t + 16 * m), v("p1", 0, 16 * m), AF.Sign, bias=v("ex", 16 * m + 15, 16 * m + 16), scale=-1.0)
-        for t, m in enumerate(TILES[0]):
-            act(slot(0, t, 16 * m), v("sg", C * t, C * t + 16 * m), AF.Sign, bias=1.0, scale=-1.0, acc=v("rs", m, m + 1))
-        tt(slot(0, 3, C), v("p0", 0, C), v("ex", 0, C), OP.is_gt)
-        joff = [0]
-        ctile(1, joff)
-        ctile(2, joff)
-        if t_ == 0:
-            setup_count()
-        qtile(1)
-        qtile(0)
-        mtile(0)
-        mtile(1)
-        ctile(3, joff)
-        qtile(2)
-        mtile(2)
-        ctile(4, joff)
-        qtile(3)
-        mtile(3)
-        ctile(5, joff)
-        qtile(4)
-        mtile(4)
-        qtile(5)
-        mtile(5)
-        tt(v("rs1", 0, 22), v("rs", 0, 22), v("cnt", 0, 22), OP.add)
-        scan(v("cs", 0, C), v("kr", 0, C), v("p2", 0, C), 0.0, OP.mult, OP.add)
-        ts(v("rs2", 0, 22), v("rs1", 0, 22), cIR, OP.mult)
-        tt(v("ru", 0, 22), v("rs2", 0, 22), v("cs", 15, C, 16), OP.subtract)
-        ts(v("roff", 0, 22), v("ru", 0, 22), cSR, OP.mult, 0.4, OP.add)
+            spread(v("ke", 0, K), 3, K)
+            act(v("gf", 0, 640), ind(v("idt", 0, PW), v("clu", 0, 40)), AF.Copy)
         cp(ind(v("win", 0, C), v("roff", 0, 22)), v("val", 0, C))
         scan(v("es", 0, K), v("ke", 0, K), v("win", 0, K), 0.0, OP.mult, OP.add)
-        ts(v("eoff", 0, 24), v("es", 3, K, 4), cSE, OP.mult, 0.1, OP.add)
-        act(v("E", 192, 384), ind(v("X", 0, 4 * C), v("eoff", 12, 24)), AF.Copy)
-        cp(v("E", 0, 192), ind(v("X", 0, 4 * C), v("eoff", 0, 12)))
+        ts(v("eoff", 0, 24), v("es", 3, K, 4), cSE, OP.mult, cT1, OP.add)
+        act(v("E", 192, 384), ind(v(X, 0, 4 * C), v("eoff", 12, 24)), AF.Copy)
+        cp(v("E", 0, 192), ind(v(X, 0, 4 * C), v("eoff", 0, 12)))
         quant("qs", "ss", 128 * sG, 128, v("E", 0, 512))
         send(sG)
         if t_ == 0:
             setup_rest()
         for b in range(4):
-            act(v("ph", PW * b, PW * b + C), v("X", b, 4 * C, 4), AF.Copy, scale=0.5)
+            act(v("ph", PW * b, PW * b + C), v(X, b, 4 * C, 4), AF.Copy, scale=0.5)
         ts(v("tw", 0, C), v("p0", 0, C), 0.0, OP.is_gt, cST, OP.mult)
-        for i in range(4):
-            ts(v("wi", 20 * i, 20 * i + 20), v("cur", 0, 20), float(7 - i), OP.add)
-        ts(v("wj", 0, 80), v("wi", 0, 80), 3, OP.bitwise_and)
-        ts(v("pt", 0, 80), v("wj", 0, 80), 2.0 ** 20, OP.mult)
         if t_ == 0:
+            act(v("ke", K, C), ind(small(3), v("rr", 0, 16)), AF.Copy)
             setup_lists()
+        else:
+            for i in range(4):
+                ts(v("wi", i, 80, 4), v("cur", 0, 20), float(7 - i), OP.add)
+            ts(v("wj", 0, 80), v("wi", 0, 80), 3, OP.bitwise_and)
+        ts(v("pt", 0, 80), v("wj", 0, 80), 2.0 ** 20, OP.mult)
         tt(v("base", 0, 80), v("pt", 0, 80), v("pay", 0, 80), OP.add)
+        tt(v("kd", 1, 80), v("base", 0, 79), v("base", 1, 80), OP.subtract)
+        ms(v("kd", 0, 80, 4), -2.0 ** 24)
         if t_ == R - 1:
             quant("qv", "sv", 0, 128, v("vb", 0, 512))
         la = 128 + K * sG - 32
@@ -410,53 +478,54 @@ def rank_program(g, core, T, topo):
         for b in range(4):
             mm("p%d" % (4 + b), "qe", "se", 128 * b, "ql", "sld", la, 128)
         ts(v("tw", C, PW), v("p3", 32, 128), 0.0, OP.is_gt, cST, OP.mult)
-        cut = 34
-        act(v("tg", 16 * cut, 1280), ind(v("tw", 0, PW), v("loff", cut, 80)), AF.Copy)
-        cp(v("tg", 0, 16 * cut), ind(v("tw", 0, PW), v("loff", 0, cut)))
+        cuts = list(zip([0] + PAR["cut"], PAR["cut"] + [80]))
+        for n, (a_, b_) in enumerate(cuts):
+            move("A" if n else "V", v("tg", 16 * a_, 16 * b_), ind(v("tw", 0, PW), v("loff", a_, b_)))
         for b in range(4):
             act(v("ph", PW * b + C, PW * b + PW), v("p%d" % (4 + b), 32, 128), AF.Copy)
-        scan(v("ts", 0, 16 * cut), v("kt", 0, 16 * cut), v("tg", 0, 16 * cut), 0.0, OP.mult, OP.add)
-        scan(v("ts", 16 * cut, 1280), v("kt", 16 * cut, 1280), v("tg", 16 * cut, 1280), 0.0, OP.mult, OP.add)
-        tt(v("key", 0, 80), v("ts", 15, 1280, 16), v("base", 0, 80), OP.add)
-        tt(v("m1", 0, 40), v("key", 0, 40), v("key", 40, 80), OP.max)
-        tt(v("mi", 0, 20), v("m1", 0, 20), v("m1", 20, 40), OP.max)
+        for (a_, b_) in cuts:
+            scan(v("ts", 16 * a_, 16 * b_), v("kt", 16 * a_, 16 * b_), v("tg", 16 * a_, 16 * b_), 0.0, OP.mult, OP.add)
+        scan(v("key", 0, 80), v("kd", 0, 80), v("ts", 15, 1280, 16), 0.0, OP.add, OP.max)
+        tt(v("mi", 0, 20), v("key", 3, 80, 4), v("base", 3, 80, 4), OP.add)
         ts(v("oti", 0, 20), v("mi", 0, 20), 511, OP.bitwise_and)
         ts(v("oti", 20, 40), v("mi", 0, 20), 9, OP.logical_shift_right, 511, OP.bitwise_and)
-        cp(v("ooff", 0, 40), v("oti", 0, 40))
-        cp(v("kg", 0, A), ind(v("kw", 0, PW), v("ooff", 0, 20)))
-        for h in range(2):
+        cp(v("ooff", 0, 20), v("oti", 0, 20))
+        cp(v("ooff", 20, 40), v("oti", 20, 40))
+        zh = PAR["zh"]
+        runs = [(0, zh), (zh, A)]
+        kg = v("mk", 0, A)
+        if not PAR["kgA"]:
+            cp(kg, ind(v("kw", 0, PW), v("ooff", 0, 20)))
+        for h, (a_, b_) in enumerate(runs):
             for b in range(4):
                 pl = v("ph", PW * b, PW * b + PW)
-                za = v("za", 640 * h + 160 * b, 640 * h + 160 * b + 160)
-                act(za, ind(pl, v("ooff", 10 * h, 10 * h + 10)), AF.Copy)
-                tt(v("Z", 640 * h + b, 640 * h + 640, 4), ind(pl, v("ooff", 20 + 10 * h, 30 + 10 * h)), za, OP.add)
-            quant("qz", "sz", 160 * h, 160, v("Z", 640 * h, 640 * h + 640))
+                za = v("za", A * b + a_, A * b + b_)
+                act(za, ind(pl, v("ooff", a_ // 16, b_ // 16)), AF.Copy)
+                tt(v("Z", 4 * a_ + b, 4 * b_, 4), ind(pl, v("ooff", 20 + a_ // 16, 20 + b_ // 16)), za, OP.add)
+            quant("qz", "sz", a_, b_ - a_, v("Z", 4 * a_, 4 * b_))
             for b in range(4):
-                mm("p%d" % ((4 + b) if h == 0 else b), "qw", "sw", 128 * b, "qz", "sz", 160 * h, 160)
-        if t_ == 0:
-            ms(v("f0", 0, 6 * FW, FW), 4096.0)
-            ms(v("f0", A, 6 * FW, FW), 160.0)
-        for c in range(6):
-            if c < 3:
-                ts(v("mk", FW * c, FW * c + A), v("kg", 0, A), float(c), OP.not_equal, 1024.0, OP.mult)
+                mm("p%d" % ((4 + b) if h == 0 else b), "qw", "sw", 128 * b, "qz", "sz", a_, b_ - a_)
+        if PAR["kgA"]:
+            act(kg, ind(v("kw", 0, PW), v("ooff", 0, 20)), AF.Copy)
+        for c in range(1, 6):
+            if c > PAR["ma"]:
+                ts(v("mk", FW * c, FW * c + A), kg, 1024.0 * c, OP.not_equal, 1024.0, OP.mult)
             else:
-                act(v("mk", FW * c, FW * c + A), v("kg", 0, A), AF.Abs, bias=col(9 + c), scale=1024.0)
-        for h in range(2):
+                act(v("mk", FW * c, FW * c + A), kg, AF.Abs, bias=col(13 + c))
+        for h, (a_, b_) in enumerate(runs):
             for b in range(4):
-                act(v("H", HW * b + 160 * h, HW * b + 160 * h + 160), v("p%d" % ((4 + b) if h == 0 else b), 0, 160),
-                    AF.Copy, scale=0.03125)
+                act(v("H", HW * b + a_, HW * b + b_), v("p%d" % ((4 + b) if h == 0 else b), 0, b_ - a_), AF.Copy, scale=0.03125)
         scan(v("fs", 0, 6 * FW), v("f0", 0, 6 * FW), v("mk", 0, 6 * FW), 0.0, OP.add, OP.min)
         ts(v("foff", 0, 6), v("fs", A, 6 * FW, FW), 159.0, OP.add, float(A), OP.min)
         for b in range(4):
-            src = ind(v("H", HW * b, HW * b + HW), v("foff", 0, 6))
-            if b < 2:
-                cp(v("V", b, 4 * K, 4), src)
-            else:
-                act(v("V", b, 4 * K, 4), src, AF.Copy)
+            move("V" if b < 2 else "A", v("V", b, 4 * K, 4), ind(v("H", HW * b, HW * b + HW), v("foff", 0, 6)))
         quant("qs", "ss", 128 * sB, 128, v("V", 0, 512))
         send(sB)
         act(v("eh", 0, 4 * K), v("E", 0, 4 * K), AF.Copy, scale=0.5)
+        tt(v("iv", 0, C), ind(v("tab", 0, C), v("roff", 0, 22)), v("val", 0, C), OP.max)
         ts(v("cur", 0, 20), v("mi", 0, 20), 18, OP.logical_shift_right, 3, OP.bitwise_and)
+        scan(v("ivs", 0, C), v("ke", 0, C), v("iv", 0, C), 0.0, OP.mult, OP.add)
+        ts(v("xoff", 0, 88), v("ivs", 3, C, 4), cSE, OP.mult, cT1, OP.add)
         if t_ == R - 1:
             cp(v("cw", 0, 20), v("cur", 0, 20))
             add("V", lambda e: e.transpose(T.cwt[:], T.cw[:]), [v("cw", 0, 32)], [v("cwt", 0, 32)])
@@ -468,22 +537,19 @@ def rank_program(g, core, T, topo):
             mm("p%d" % (4 + b), "qe", "se", 128 * b, "ql", "sld", la, 128,
                waits=[("arr%d" % sB, arrivals(sB, rank, T, topo))] if b == 0 else [])
         for b in range(4):
-            tt(v("upd", b, 4 * K, 4), v("p%d" % (4 + b), 32, 128), v("eh", b, 4 * K, 4), OP.add)
-        cp(ind(v("X", 0, 4 * C), v("eoff", 0, 24)), v("upd", 0, 4 * K))
+            tt(v(X, 4 * C + b, 4 * PW, 4), v("p%d" % (4 + b), 32, 128), v("eh", b, 4 * K, 4), OP.add)
+        act(v(Xn, 0, 4 * LO), ind(v(X, 0, 4 * PW), v("xoff", 0, LO // 4)), AF.Copy)
+        cp(v(Xn, 4 * LO, 4 * C), ind(v(X, 0, 4 * PW), v("xoff", LO // 4, C // 4)))
 
-    quant("qx", "sx", 0, C, v("X", 0, 4 * C))
-    mm("p0", "qv", "sv", 0, "qx", "sx", 0, C)
-    dma("S", T.oc[:], T.qx[:].bitcast(dt.uint8), [v("qx", 0, C)], [])
+    for (a, b, bank, eng) in ((LO, C, "p3", "A"), (0, LO, "p0", "V")):
+        quant("qx", "sx", a, b - a, v(Xn, 4 * a, 4 * b))
+        mm(bank, "qv", "sv", 0, "qx", "sx", a, b - a)
+        dma("S", T.oc[:, 4 * a:4 * b], T.qx[:, a:b].bitcast(dt.uint8), [v("qx", a, b)], [])
     for k in range(4):
-        dma("A", T.osc[4 * k:4 * k + 4, :], T.sx[32 * k:32 * k + 4, :], [v("sx", 0, C)], [])
-    cp(v("yb", 0, C), v("p0", 0, C))
-    dma("S", T.y[:], T.yb[:], [v("yb", 0, C)], [])
-
-    tail = ops[:]
-    del ops[:]
-    for c in range(3, 6):
-        ms(col(9 + c), -1024.0 * c)
-    ops.extend(tail)
+        dma("S", T.osc[4 * k:4 * k + 4, :], T.sx[32 * k:32 * k + 4, :], [v("sx", 0, C)], [])
+    for (a, b, bank, eng) in ((LO, C, "p3", "A"), (0, LO, "p0", "V")):
+        move(eng, v("yb", a, b), v(bank, 0, b - a))
+        dma("A", T.y[:, a:b], T.yb[:, a:b], [v("yb", a, b)], [])
     emit(g, T, ops, sent[0])
 
 

from concourse.bass import DstId, RemoteDMATransfer
from concourse.mybir import dt, AluOpType, ActivationFunctionType

C, K, A, R = 352, 96, 320, 3
PW = C + K
HW = 336
FW = A + 1
BIG = 1e29
TILES = [[21, 20, 19], [18, 17, 16, 15], [14, 13, 12, 11], [10, 9, 8, 7], [6, 5, 4, 3], [2, 1]]
TWID = [352, 288, 224, 160, 128, 128]
TOFF = [sum(TWID[:i]) for i in range(6)]
X4, U8 = "float8_e4m3fn_x4", "uint8"
LO = 192
PAR = {"nb": 5, "e": (5, 6, 7, 8, 9, 10), "cut": [30, 68], "zh": 160, "ma": 3, "kgA": False,
       "qord": [(2, 3), (0, 3), (3, 4), (1, 4), (4, 5), (5, 5)]}


def _sb(n, d):
    return ("sbuf", [128, n], d)


SCRATCH = {
    "Xa": _sb(4 * PW, "bfloat16"), "Xb": _sb(4 * PW, "bfloat16"), "qx": _sb(C, X4), "sx": _sb(C, U8),
    "ub": _sb(512, "bfloat16"), "qu0": _sb(128, X4), "su0": _sb(128, U8), "qu": _sb(128, X4), "su": _sb(128, U8),
    "vb": _sb(512, "bfloat16"), "qv": _sb(128, X4), "sv": _sb(128, U8),
    "qw": _sb(512, X4), "sw": _sb(512, U8),
    "cli": _sb(80, "int32"), "clu": _sb(80, "uint16"),
    "pint": _sb(8, "int32"), "cf": _sb(20, "float32"), "uoi": _sb(40, "int32"), "uoff": _sb(40, "uint16"),
    "idt": _sb(PW, "float32"), "j16": _sb(K, "float32"), "j4": _sb(16, "float32"), "k1": _sb(K, "float32"),
    "sm": _sb(96, "float32"), "rr": _sb(22, "uint16"), "eb": _sb(516, "bfloat16"),
    "ab": _sb(512, "bfloat16"), "a0b": _sb(512, "bfloat16"), "zb": _sb(516, "bfloat16"),
    "qa": _sb(256, X4), "sa": _sb(256, U8), "qe": _sb(512, X4), "se": _sb(512, U8),
    "msel": _sb(C, "float32"), "mres": _sb(C, "float32"), "kr": _sb(C, "float32"), "ktm": _sb(K, "float32"),
    "ktn": _sb(K, "float32"), "kt": _sb(1280, "bfloat16"), "ke": _sb(C, "float32"), "val": _sb(C, "float32"),
    "tab": _sb(C, "float32"), "iv": _sb(C, "float32"), "ivs": _sb(C, "float32"), "xoff": _sb(88, "uint16"),
    "cnt": _sb(22, "float32"), "kw": _sb(PW, "bfloat16"), "f0": _sb(6 * FW, "bfloat16"),
    "gf": _sb(1280, "float32"), "sl": _sb(1280, "float32"), "li": _sb(80, "int32"), "loff": _sb(80, "uint16"),
    "pay": _sb(80, "float32"), "pt": _sb(80, "float32"), "cur": _sb(20, "int32"), "wi": _sb(80, "int32"),
    "wj": _sb(80, "int32"), "base": _sb(80, "float32"), "kd": _sb(80, "float32"),
    "t1": _sb(C, "float32"), "ex": _sb(C, "float32"), "ct": _sb(4 * 1280, "bfloat16"),
    "qc": _sb(1280, X4), "sc": _sb(1280, U8), "sg": _sb(2400, "bfloat16"), "junk": _sb(3072 + 16 * 256, "bfloat16"),
    "one": _sb(256, "bfloat16"),
    "rs": _sb(22, "float32"), "rs1": _sb(22, "float32"), "rs2": _sb(22, "float32"), "cs": _sb(C, "float32"),
    "ru": _sb(22, "float32"), "roff": _sb(22, "uint16"), "win": _sb(C, "float32"), "es": _sb(K, "float32"),
    "eoff": _sb(24, "uint16"), "E": _sb(512, "bfloat16"), "eh": _sb(4 * K, "bfloat16"),
    "qs": _sb(6 * 128, X4), "ss": _sb(6 * 128, U8), "ql": _sb(128 + 6 * K, X4), "sld": _sb(128 + 6 * K, U8),
    "ph": _sb(4 * PW, "bfloat16"), "tw": _sb(PW, "bfloat16"), "tg": _sb(1280, "bfloat16"), "ts": _sb(1280, "bfloat16"),
    "key": _sb(80, "float32"), "mi": _sb(20, "int32"), "oti": _sb(40, "int32"),
    "ooff": _sb(40, "uint16"), "za": _sb(1280, "bfloat16"), "Z": _sb(1280, "bfloat16"), "qz": _sb(A, X4), "sz": _sb(A, U8),
    "H": _sb(4 * HW, "bfloat16"), "mk": _sb(6 * FW, "bfloat16"), "fs": _sb(6 * FW, "bfloat16"),
    "foff": _sb(6, "uint16"), "V": _sb(512, "bfloat16"),
    "cw": _sb(32, "float32"), "cwt": _sb(32, "float32"), "yb": _sb(C, "float32"),
}
for _b in range(8):
    SCRATCH["p%d" % _b] = ("psum", [128, 512], "float32")
NDMA = 28
SEMAPHORES = (["eV", "eA", "eT", "eG", "snt"] + ["arr%d" % _s for _s in range(6)] + ["d%d" % _s for _s in range(NDMA)])

OP, AF = AluOpType, ActivationFunctionType


def v(name, a, b, s=1):
    return (name, a, b, s)


def ind(win, off):
    return ("*", win, off)


def bits(x):
    m = 0
    if x[3] == 1:
        return ((1 << (x[2] - x[1])) - 1) << x[1]
    for c in range(x[1], x[2], x[3]):
        m |= 1 << c
    return m


def mask_of(es):
    m = 0
    for e in es:
        m |= 1 << e
    return m


def ends(s, rank, T):
    n = len(T.cores)
    d = 1 if s % 2 == 0 else -1
    return T.cores[rank], T.cores[(rank + d) % n]


def pieces(src, dst, T, topo):
    if topo.may_write(src, dst):
        a = b = dst
    else:
        c = [k for k in topo.cores_of(src) if topo.may_write(k, dst) and T.rank_of(k) is None]
        a = [k for k in c if topo.die(k) == topo.die(src)][0]
        b = [k for k in c if topo.die(k) != topo.die(src)][0]
    return [[(a, 0, 0, K, topo.engines(src, a))], [(b, 1, 0, K, topo.engines(src, b))]]


def land(T, s, which, a, b):
    o = 128 + K * s
    return T.ql[:, o + a:o + b].bitcast(dt.uint8) if which == 0 else T.sld[:, o + a:o + b]


def arrivals(s, rank, T, topo):
    n = len(T.cores)
    src, dst = ends(s, (rank - (1 if s % 2 == 0 else -1)) % n, T)
    return sum(len(p[4]) if p[0] == dst else len(topo.engines(p[0], dst)) for call in pieces(src, dst, T, topo) for p in call)


def relay_program(g, core, T, topo):
    total = 0
    for s in range(6):
        for r in range(len(T.cores)):
            src, dst = ends(s, r, T)
            for call in pieces(src, dst, T, topo):
                for (via, w, a, b, es) in call:
                    if via == core:
                        g.wait_ge(T.sem["arr%d" % s], len(es))
                        rid, pid = topo.addr(dst, core)
                        g.remote_dma(land(T, s, w, a, b), land(T, s, w, a, b), T.sem["arr%d" % s], T.sem.snt, pid, rid,
                                     topo.mask(core, dst))
                        total += len(topo.engines(core, dst))
    if total:
        g.wait_ge(T.sem.snt, total)


def rank_program(g, core, T, topo):
    rank = T.rank_of(core)
    if rank is None:
        relay_program(g, core, T, topo)
        return
    ops = []
    ndma = [0]
    sent = [0]

    def ap(x):
        if not isinstance(x, tuple):
            return x
        if x[0] == "*":
            return ap(x[1]).indirect(ap(x[2]))
        return T[x[0]][:, x[1]:x[2]] if x[3] == 1 else T[x[0]][:, x[1]:x[2]:x[3]]

    def add(eng, fn, rd, wr, waits=(), dma=False):
        r, w = [], []
        for x in rd:
            if isinstance(x, tuple):
                r += [x[1], x[2]] if x[0] == "*" else [x]
        for x in wr:
            if x[0] == "*":
                w.append(x[1])
                r.append(x[2])
            else:
                w.append(x)
        o = {"eng": eng, "fn": fn, "r": [(x[0], bits(x)) for x in r], "w": [(x[0], bits(x)) for x in w],
             "waits": list(waits), "dma": None}
        if dma:
            o["dma"] = "d%d" % ndma[0]
            ndma[0] += 1
        ops.append(o)

    def ts(out, in0, s1, op0, s2=None, op1=None):
        if op1 is None:
            add("V", lambda e: e.tensor_scalar(ap(out), ap(in0), ap(s1), None, op0), [in0, s1], [out])
        else:
            add("V", lambda e: e.tensor_scalar(ap(out), ap(in0), ap(s1), ap(s2), op0, op1), [in0, s1, s2], [out])

    def tt(out, a, b, op):
        add("V", lambda e: e.tensor_tensor(ap(out), ap(a), ap(b), op), [a, b], [out])

    def cp(out, a):
        add("V", lambda e: e.tensor_copy(ap(out), ap(a)), [a], [out])

    def ms(out, c):
        add("V", lambda e: e.memset(ap(out), c), [], [out])

    def scan(out, d0, d1, init, op0, op1):
        add("V", lambda e: e.tensor_tensor_scan(ap(out), ap(d0), ap(d1), init, op0, op1), [d0, d1], [out])

    def act(out, a, func, bias=None, scale=None, acc=None):
        kw = {}
        if bias is not None:
            kw["bias"] = ap(bias)
        if scale is not None:
            kw["scale"] = ap(scale)
        if acc is not None:
            kw["accum_out"] = ap(acc)
        add("A", lambda e: e.activation(ap(out), ap(a), func, **kw), [a, bias, scale], [out] + ([acc] if acc else []))

    def move(eng, out, a, scale=None):
        if eng == "A":
            act(out, a, AF.Copy, scale=scale)
        elif scale is None:
            cp(out, a)
        else:
            ts(out, a, scale, OP.mult)

    def quant(q, s, a, n, src):
        add("V", lambda e: e.quantize_mx(T[q][:, a:a + n], T[s][:, a:a + n], ap(src)), [src], [v(q, a, a + n), v(s, a, a + n)])

    def mm(bank, lq, ls, la, rq, rs_, ra, n, start=True, stop=True, waits=()):
        add("T", lambda e: e.matmul_mx(T[bank][:, 0:n], T[lq][:, la:la + 128], T[ls][:, la:la + 128],
                                       T[rq][:, ra:ra + n], T[rs_][:, ra:ra + n], start, stop),
            [v(lq, la, la + 128), v(ls, la, la + 128), v(rq, ra, ra + n), v(rs_, ra, ra + n)], [v(bank, 0, n)], waits)

    def iota(out, pat, base, cm, flt=True):
        if flt:
            add("G", lambda e: e.iota(ap(out), pat, base, cm, allow_small_or_imprecise_dtypes=True), [], [out])
        else:
            add("G", lambda e: e.iota(ap(out), pat, base, cm), [], [out])

    def fill(out, c):
        iota(out, [[0, len(range(*out[1:]))]], c, 0)

    def diagonal(out, src, n, fill_):
        add("G", lambda e: e.affine_select(ap(out), ap(src), [[1, n]], OP.not_equal, fill_, -3, -4), [src], [out])

    def dma(eng, out, in_, rd, wr):
        add(eng, lambda e: e.dma_start(out, in_), rd, wr, dma=True)

    def send(s):
        src, dst = ends(s, rank, T)
        for call in pieces(src, dst, T, topo):
            tr, rd = [], []
            for (via, w, a, b, es) in call:
                o = 128 * s
                frm = T.qs[:, o + a:o + b].bitcast(dt.uint8) if w == 0 else T.ss[:, o + a:o + b]
                sent[0] += len(es)
                tr.append((land(T, s, w, a, b), frm, topo.addr(via, src), mask_of(es)))
                rd.append(v("qs" if w == 0 else "ss", o + a, o + b))
            if len(tr) == 1:
                to, frm, (rid, pid), m = tr[0]
                add("G", lambda e, to=to, frm=frm, rid=rid, pid=pid, m=m: e.remote_dma(
                    to, frm, T.sem["arr%d" % s], T.sem.snt, pid, rid, m), rd, [])
            else:
                add("G", lambda e, tr=tr: e.remote_dma_fused(
                    [RemoteDMATransfer(dst_ids=[DstId(rid=rid, pnc=pid)], dma_engine_mask=m, remote_sem=T.sem["arr%d" % s],
                                       src=frm, dst=to) for (to, frm, (rid, pid), m) in tr], local_sem=T.sem.snt), rd, [])

    def col(i):
        return v("cf", i, i + 1)
    cR, cG, cT, cQ, cR1, cQ1, cSR, cIR, cSE, cST, cA, cB, cT1, cK = [col(i) for i in range(14)]
    cNI = col(19)

    def small(i):
        return v("sm", 16 * i, 16 * i + 16)

    def spread(out, i, n):
        act(out, ind(small(i), v("rr", 0, n // 16)), AF.Copy)

    def horner(i, jt, c0, c1, big):
        ts(v("ktm", 16 * i, 16 * i + 16), v(jt, 0, 16), c0, OP.not_equal)
        ts(v("ktn", 16 * i, 16 * i + 16), v(jt, 0, 16), c1, OP.is_equal, big - 1.0, OP.mult)

    def pad(i):
        lo = 16 * TILES[i][-1] if i < 5 else 0
        fill(v("ct", 4 * (TOFF[i] + lo), 4 * (TOFF[i] + TWID[i])), 0)

    dma("S", T.Xa[:, 4 * LO:4 * C], T.x[:, 4 * LO:4 * C], [], [v("Xa", 4 * LO, 4 * C)])
    dma("A", T.ub[:], T.u[:], [], [v("ub", 0, 512)])
    dma("S", T.Xa[:, 0:4 * LO], T.x[:, 0:4 * LO], [], [v("Xa", 0, 4 * LO)])
    dma("S", T.cli[:], T.cl[:], [], [v("cli", 0, 80)])
    dma("S", T.qw[:].bitcast(dt.uint8), T.wc[:], [], [v("qw", 0, 512)])
    dma("S", T.sw[:], T.ws[:], [], [v("sw", 0, 512)])
    dma("S", T.vb[:], T.v[:], [], [v("vb", 0, 512)])

    iota(v("pint", 0, 1), [[1, 1]], 0, 1, False)
    iota(v("j16", 0, 32), [[0, 2], [1, 16]], 0, 0)
    iota(v("uoi", 8, 40), [[1, 8], [0, 4]], 0, 0, False)
    iota(v("uoi", 0, 8), [[16, 8]], 0, 0, False)
    iota(v("j4", 0, 16), [[0, 4], [1, 4]], 0, 0)
    iota(v("cnt", 0, 22), [[16, 22]], 0, 0)
    fill(v("rs2", 0, 1), 0)
    pad(0)
    pi = v("pint", 0, 1)
    ts(v("pint", 1, 2), pi, 15, OP.bitwise_and)
    ts(v("pint", 2, 3), pi, 4, OP.logical_shift_right)
    ts(v("pint", 3, 4), pi, 3, OP.bitwise_and)
    ts(v("pint", 4, 5), pi, 2, OP.logical_shift_right, 3, OP.bitwise_and)
    cp(v("cf", 0, 4), v("pint", 1, 5))
    cp(v("uoff", 0, 40), v("uoi", 0, 40))
    ts(small(5), v("j16", 0, 16), cG, OP.is_equal)
    ts(v("rr", 0, 22), v("j16", 0, 22), 0.0, OP.mult, cR, OP.add)
    ts(small(0), v("j16", 0, 16), cR, OP.not_equal, BIG, OP.mult)
    ms(v("mres", 0, C), 0.0)
    act(v("ab", 0, 512), ind(small(5), v("uoff", 8, 40)), AF.Copy)
    spread(v("msel", 0, C), 0, C)
    diagonal(v("a0b", 0, 512), v("ab", 0, 512), 512, -16384.0)
    ts(cR1, cR, 1.0, OP.add)
    ts(cQ1, cQ, 1.0, OP.add)
    ts(cSR, cR, 15.0, OP.is_equal, 2.0 ** -14, OP.max)
    ts(cA, cR, 15.0, OP.not_equal, 2.0 ** 14, OP.mult)
    horner(2, "j16", cR, cR1, 2.0 ** 14)
    horner(3, "j4", cQ, cQ1, 2.0 ** 14)
    ts(cSE, cQ, 3.0, OP.is_equal, 2.0 ** -14, OP.max)
    ts(cIR, cA, 1.0, OP.max)
    ts(cT1, cT, 0.1, OP.add)
    tt(v("sm", 32, 64), v("ktm", 32, 64), v("ktn", 32, 64), OP.add)
    ts(cK, cR, C - 16 + 0.4, OP.add)
    ts(cNI, cIR, -1.0, OP.mult)
    ms(v("mres", 0, C, 16), BIG)
    quant("qa", "sa", 128, 128, v("ab", 0, 512))
    quant("qu0", "su0", 0, 128, v("ub", 0, 512))
    add("A", lambda e: e.activation(T.su[:], T.su0[:].indirect(T.uoff[:, 0:8]), AF.Copy),
        [v("su0", 0, 128), v("uoff", 0, 8)], [v("su", 0, 128)])
    add("V", lambda e: e.tensor_copy(T.qu[:].bitcast(dt.uint32), T.qu0[:].bitcast(dt.uint32).indirect(T.uoff[:, 0:8])),
        [v("qu0", 0, 128), v("uoff", 0, 8)], [v("qu", 0, 128)])
    spread(v("kr", 0, C), 2, C)
    for i in range(1, 6):
        pad(i)
    if PAR["e"]:
        fill(v("one", 0, 16 * max(PAR["e"])), 1)
    iota(v("idt", 0, PW), [[1, PW]], 0, 0)
    iota(v("val", 0, C), [[4, C]], 0, 0)
    fill(v("E", 4 * K, 512), 0)
    fill(v("zb", 0, 516), 0)
    diagonal(v("eb", 0, 516), v("zb", 0, 516), 516, 0.5)

    def setup_rest():
        iota(v("wj", 0, 80), [[0, 20], [-1, 4]], 3, 0, False)
        iota(v("j16", 32, K), [[0, 4], [1, 16]], 0, 0)
        iota(v("k1", 0, K), [[1024, 6], [0, 16]], -8192, 0)
        fill(v("kw", 0, C), 8192)
        iota(v("cf", 14, 19), [[-1024, 5]], -1024, 0)
        fill(v("mk", A, 6 * FW, FW), 4096)
        fill(v("H", A, 4 * HW, HW), 0)
        fill(v("V", 4 * K, 512), 0)
        fill(v("f0", 0, 6 * FW), -1)
        fill(v("f0", 0, 6 * FW, FW), 4096)
        fill(v("f0", A, 6 * FW, FW), 160)
        iota(v("tab", 0, K), [[4, K]], 4 * C, 0)
        fill(v("tab", K, C), 0)
        fill(v("cw", 20, 32), 0)
        act(v("gf", 640, 1280), ind(v("idt", 0, PW), v("clu", 40, 80)), AF.Copy)
        horner(4, "j16", cR, cR1, 2.0 ** 28)
        ts(cB, cR, 15.0, OP.is_equal, 2.0 ** 22, OP.mult)
        tt(small(4), v("ktm", 64, 80), v("ktn", 64, 80), OP.add)
        ts(cST, cB, 2.0 ** -6, OP.max)
        spread(v("kt", 0, A), 4, A)
        act(v("kt", A, 2 * A), v("kt", 0, A), AF.Copy)
        act(v("kt", 2 * A, 4 * A), v("kt", 0, 2 * A), AF.Copy)
        quant("ql", "sld", 0, 128, v("zb", 0, 512))
        for b in range(4):
            quant("qe", "se", 128 * b, 128, v("eb", 3 - b, 515 - b))

    def setup_lists():
        for i in range(4):
            scan(v("sl", A * i, A * i + A), v("kr", 0, A), v("gf", i, 1280, 4), 0.0, OP.mult, OP.add)
        ts(v("ktm", 0, K), v("j16", 0, K), cR, OP.is_equal)
        for i in range(4):
            ts(v("li", i, 80, 4), v("sl", A * i + 15, A * i + A, 16), cSR, OP.mult)
        tt(v("ktn", 0, K), v("ktm", 0, K), v("k1", 0, K), OP.mult)
        cp(v("loff", 0, 80), v("li", 0, 80))
        ts(v("kw", C, PW), v("ktn", 0, K), 8192.0, OP.add)
        for i in range(4):
            ts(v("pay", i, 80, 4), v("li", (i + 1) % 4, 80, 4), 512.0, OP.mult, float(i << 18), OP.add)
        tt(v("pay", 0, 80), v("pay", 0, 80), v("li", 0, 80), OP.add)

    def slot(i, t, a, b):
        return v("ct", 4 * (TOFF[i] + a) + t, 4 * (TOFF[i] + b), 4)

    WHERE = {m: (i, t) for i in range(6) for t, m in enumerate(TILES[i])}
    BOTH = list(range(21, 21 - PAR["nb"], -1))
    SCAN = list(PAR["e"])

    def pivot(m):
        return v("ex", 16 * m + 15, 16 * m + 16)

    def qtile(i):
        quant("qc", "sc", TOFF[i], TWID[i], v("ct", 4 * TOFF[i], 4 * (TOFF[i] + TWID[i])))

    def compare(m):
        ts(slot(*WHERE[m], 0, 16 * m), v("p0", 0, 16 * m), pivot(m), OP.is_ge)

    def rowsum(m):
        e_ = 3072 + 256 * (m - min(SCAN)) + 256
        scan(v("junk", e_ - 16 * m, e_), v("one", 0, 16 * m), slot(*WHERE[m], 0, 16 * m), -16.0 * m, OP.mult, OP.add)

    def order(X, first):
        quant("qx", "sx", LO, C - LO, v(X, 4 * LO, 4 * C))
        mm("p3", "qu", "su", 0, "qx", "sx", LO, C - LO)
        quant("qx", "sx", 0, LO, v(X, 0, 4 * LO))
        mm("p1", "qu", "su", 0, "qx", "sx", 0, C - 16)
        mm("p0", "qu", "su", 0, "qx", "sx", 0, C)
        tt(v("t1", LO, C), v("p3", 0, C - LO), v("msel", LO, C), OP.add)
        scan(v("ex", LO, C), v("mres", LO, C), v("t1", LO, C), 0.0, OP.add, OP.min)
        if first:
            quant("qa", "sa", 0, 128, v("a0b", 0, 512))
            cp(v("clu", 0, 80), v("cli", 0, 80))
        tt(slot(0, 3, LO, C), v("p3", 0, C - LO), v("ex", LO, C), OP.is_gt)
        tt(v("t1", 0, LO), v("p0", 0, LO), v("msel", 0, LO), OP.add)
        lead = [m for m in range(21, LO // 16 - 1, -1) if m not in BOTH][0]
        compare(lead)
        scan(v("ex", 0, LO), v("mres", 0, LO), v("t1", 0, LO), 0.0, OP.add, OP.min)
        so = 0
        for k in range(0, len(BOTH), 2):
            pair = [(m, so + sum(16 * n for n in BOTH[k:k + 2] if n > m)) for m in BOTH[k:k + 2]]
            for m, o in pair:
                act(v("sg", o, o + 16 * m), v("p1", 0, 16 * m), AF.Sign, bias=pivot(m), scale=-1.0)
            for m, o in pair:
                act(slot(*WHERE[m], 0, 16 * m), v("sg", o, o + 16 * m), AF.Sign, bias=1.0, scale=-1.0, acc=v("rs", m, m + 1))
            so += sum(16 * n for n in BOTH[k:k + 2])
        done, jo, ready, summed = [], 0, [], []
        for i in range(6):
            for m in TILES[i]:
                if m in BOTH:
                    continue
                s_ = slot(*WHERE[m], 0, 16 * m)
                if m != lead:
                    compare(m)
                if not done and m != lead:
                    done.append(m)
                    tt(slot(0, 3, 0, LO), v("p0", 0, LO), v("ex", 0, LO), OP.is_gt)
                if m not in SCAN:
                    act(v("junk", jo, jo + 16 * m), s_, AF.Identity, bias=cNI, scale=cIR, acc=v("rs2", m, m + 1))
                    jo += 16 * m
            for m in TILES[i]:
                if m in SCAN and i < 5:
                    rowsum(m)
            for (q, after) in PAR["qord"]:
                if after == i:
                    qtile(q)
                    ready.append(q)
                    while 0 in ready + summed and ready:
                        n = 0 if 0 in ready else ready[0]
                        ready.remove(n)
                        summed.append(n)
                        mm("p2", "qa", "sa", 0 if n == 0 else 128, "qc", "sc", TOFF[n], TWID[n], n == 0, len(summed) == 6)
        lo = min(BOTH)
        tt(v("rs1", lo, 22), v("rs", lo, 22), v("cnt", lo, 22), OP.subtract)
        for m in TILES[5]:
            if m in SCAN:
                rowsum(m)
        ts(v("rs2", lo, 22), v("rs1", lo, 22), cIR, OP.mult)
        if SCAN:
            a_, b_ = min(SCAN), max(SCAN) + 1
            ts(v("rs2", a_, b_), v("junk", 3072 + 255, 3072 + 256 * (b_ - a_), 256), cIR, OP.mult)
        scan(v("cs", 0, C), v("kr", 0, C), v("p2", 0, C), 0.0, OP.mult, OP.add)
        tt(v("ru", 0, 22), v("rs2", 0, 22), v("cs", 15, C, 16), OP.subtract)
        ts(v("roff", 0, 22), v("ru", 0, 22), cSR, OP.mult, cK, OP.add)

    for t_ in range(R):
        sG, sB = 2 * t_, 2 * t_ + 1
        X, Xn = ("Xa", "Xb") if t_ % 2 == 0 else ("Xb", "Xa")
        order(X, t_ == 0)
        if t_ == 0:
            spread(v("ke", 0, K), 3, K)
            act(v("gf", 0, 640), ind(v("idt", 0, PW), v("clu", 0, 40)), AF.Copy)
        cp(ind(v("win", 0, C), v("roff", 0, 22)), v("val", 0, C))
        scan(v("es", 0, K), v("ke", 0, K), v("win", 0, K), 0.0, OP.mult, OP.add)
        ts(v("eoff", 0, 24), v("es", 3, K, 4), cSE, OP.mult, cT1, OP.add)
        act(v("E", 192, 384), ind(v(X, 0, 4 * C), v("eoff", 12, 24)), AF.Copy)
        cp(v("E", 0, 192), ind(v(X, 0, 4 * C), v("eoff", 0, 12)))
        quant("qs", "ss", 128 * sG, 128, v("E", 0, 512))
        send(sG)
        if t_ == 0:
            setup_rest()
        for b in range(4):
            act(v("ph", PW * b, PW * b + C), v(X, b, 4 * C, 4), AF.Copy, scale=0.5)
        ts(v("tw", 0, C), v("p0", 0, C), 0.0, OP.is_gt, cST, OP.mult)
        if t_ == 0:
            act(v("ke", K, C), ind(small(3), v("rr", 0, 16)), AF.Copy)
            setup_lists()
        else:
            for i in range(4):
                ts(v("wi", i, 80, 4), v("cur", 0, 20), float(7 - i), OP.add)
            ts(v("wj", 0, 80), v("wi", 0, 80), 3, OP.bitwise_and)
        ts(v("pt", 0, 80), v("wj", 0, 80), 2.0 ** 20, OP.mult)
        tt(v("base", 0, 80), v("pt", 0, 80), v("pay", 0, 80), OP.add)
        tt(v("kd", 1, 80), v("base", 0, 79), v("base", 1, 80), OP.subtract)
        ms(v("kd", 0, 80, 4), -2.0 ** 24)
        if t_ == R - 1:
            quant("qv", "sv", 0, 128, v("vb", 0, 512))
        la = 128 + K * sG - 32
        mm("p3", "qu", "su", 0, "ql", "sld", la, 128, waits=[("arr%d" % sG, arrivals(sG, rank, T, topo))])
        for b in range(4):
            mm("p%d" % (4 + b), "qe", "se", 128 * b, "ql", "sld", la, 128)
        ts(v("tw", C, PW), v("p3", 32, 128), 0.0, OP.is_gt, cST, OP.mult)
        cuts = list(zip([0] + PAR["cut"], PAR["cut"] + [80]))
        for n, (a_, b_) in enumerate(cuts):
            move("A" if n else "V", v("tg", 16 * a_, 16 * b_), ind(v("tw", 0, PW), v("loff", a_, b_)))
        for b in range(4):
            act(v("ph", PW * b + C, PW * b + PW), v("p%d" % (4 + b), 32, 128), AF.Copy)
        for (a_, b_) in cuts:
            scan(v("ts", 16 * a_, 16 * b_), v("kt", 16 * a_, 16 * b_), v("tg", 16 * a_, 16 * b_), 0.0, OP.mult, OP.add)
        scan(v("key", 0, 80), v("kd", 0, 80), v("ts", 15, 1280, 16), 0.0, OP.add, OP.max)
        tt(v("mi", 0, 20), v("key", 3, 80, 4), v("base", 3, 80, 4), OP.add)
        ts(v("oti", 0, 20), v("mi", 0, 20), 511, OP.bitwise_and)
        ts(v("oti", 20, 40), v("mi", 0, 20), 9, OP.logical_shift_right, 511, OP.bitwise_and)
        cp(v("ooff", 0, 20), v("oti", 0, 20))
        cp(v("ooff", 20, 40), v("oti", 20, 40))
        zh = PAR["zh"]
        runs = [(0, zh), (zh, A)]
        kg = v("mk", 0, A)
        if not PAR["kgA"]:
            cp(kg, ind(v("kw", 0, PW), v("ooff", 0, 20)))
        for h, (a_, b_) in enumerate(runs):
            for b in range(4):
                pl = v("ph", PW * b, PW * b + PW)
                za = v("za", A * b + a_, A * b + b_)
                act(za, ind(pl, v("ooff", a_ // 16, b_ // 16)), AF.Copy)
                tt(v("Z", 4 * a_ + b, 4 * b_, 4), ind(pl, v("ooff", 20 + a_ // 16, 20 + b_ // 16)), za, OP.add)
            quant("qz", "sz", a_, b_ - a_, v("Z", 4 * a_, 4 * b_))
            for b in range(4):
                mm("p%d" % ((4 + b) if h == 0 else b), "qw", "sw", 128 * b, "qz", "sz", a_, b_ - a_)
        if PAR["kgA"]:
            act(kg, ind(v("kw", 0, PW), v("ooff", 0, 20)), AF.Copy)
        for c in range(1, 6):
            if c > PAR["ma"]:
                ts(v("mk", FW * c, FW * c + A), kg, 1024.0 * c, OP.not_equal, 1024.0, OP.mult)
            else:
                act(v("mk", FW * c, FW * c + A), kg, AF.Abs, bias=col(13 + c))
        for h, (a_, b_) in enumerate(runs):
            for b in range(4):
                act(v("H", HW * b + a_, HW * b + b_), v("p%d" % ((4 + b) if h == 0 else b), 0, b_ - a_), AF.Copy, scale=0.03125)
        scan(v("fs", 0, 6 * FW), v("f0", 0, 6 * FW), v("mk", 0, 6 * FW), 0.0, OP.add, OP.min)
        ts(v("foff", 0, 6), v("fs", A, 6 * FW, FW), 159.0, OP.add, float(A), OP.min)
        for b in range(4):
            move("V" if b < 2 else "A", v("V", b, 4 * K, 4), ind(v("H", HW * b, HW * b + HW), v("foff", 0, 6)))
        quant("qs", "ss", 128 * sB, 128, v("V", 0, 512))
        send(sB)
        act(v("eh", 0, 4 * K), v("E", 0, 4 * K), AF.Copy, scale=0.5)
        tt(v("iv", 0, C), ind(v("tab", 0, C), v("roff", 0, 22)), v("val", 0, C), OP.max)
        ts(v("cur", 0, 20), v("mi", 0, 20), 18, OP.logical_shift_right, 3, OP.bitwise_and)
        scan(v("ivs", 0, C), v("ke", 0, C), v("iv", 0, C), 0.0, OP.mult, OP.add)
        ts(v("xoff", 0, 88), v("ivs", 3, C, 4), cSE, OP.mult, cT1, OP.add)
        if t_ == R - 1:
            cp(v("cw", 0, 20), v("cur", 0, 20))
            add("V", lambda e: e.transpose(T.cwt[:], T.cw[:]), [v("cw", 0, 32)], [v("cwt", 0, 32)])
            for gg in range(8):
                a, h = gg // 2, gg % 2
                dma("S", T.ow[gg:gg + 1, :], T.cwt[32 * a:32 * a + 20, 16 * h:16 * h + 16], [v("cwt", 0, 32)], [])
        la = 128 + K * sB - 32
        for b in range(4):
            mm("p%d" % (4 + b), "qe", "se", 128 * b, "ql", "sld", la, 128,
               waits=[("arr%d" % sB, arrivals(sB, rank, T, topo))] if b == 0 else [])
        for b in range(4):
            tt(v(X, 4 * C + b, 4 * PW, 4), v("p%d" % (4 + b), 32, 128), v("eh", b, 4 * K, 4), OP.add)
        act(v(Xn, 0, 4 * LO), ind(v(X, 0, 4 * PW), v("xoff", 0, LO // 4)), AF.Copy)
        cp(v(Xn, 4 * LO, 4 * C), ind(v(X, 0, 4 * PW), v("xoff", LO // 4, C // 4)))

    for (a, b, bank, eng) in ((LO, C, "p3", "A"), (0, LO, "p0", "V")):
        quant("qx", "sx", a, b - a, v(Xn, 4 * a, 4 * b))
        mm(bank, "qv", "sv", 0, "qx", "sx", a, b - a)
        dma("S", T.oc[:, 4 * a:4 * b], T.qx[:, a:b].bitcast(dt.uint8), [v("qx", a, b)], [])
    for k in range(4):
        dma("S", T.osc[4 * k:4 * k + 4, :], T.sx[32 * k:32 * k + 4, :], [v("sx", 0, C)], [])
    for (a, b, bank, eng) in ((LO, C, "p3", "A"), (0, LO, "p0", "V")):
        move(eng, v("yb", a, b), v(bank, 0, b - a))
        dma("A", T.y[:, a:b], T.yb[:, a:b], [v("yb", a, b)], [])
    emit(g, T, ops, sent[0])


def emit(g, T, ops, sent):
    q = {"V": g.vector, "A": g.scalar, "T": g.tensor, "G": g, "S": g.sync}
    known = {e: {} for e in q}
    hist = {}
    need = set()
    for i, o in enumerate(ops):
        deps = set()
        for kind in ("r", "w"):
            for name, m in o[kind]:
                bank = SCRATCH[name][0] == "psum"
                for (j, jm, jw) in hist.get(name, []):
                    same = ops[j]["eng"] == o["eng"] and ops[j]["dma"] is None and o["dma"] is None
                    if bank:
                        if not same:
                            deps.add(j)
                    elif (jm & m) and (jw or kind == "w"):
                        deps.add(j)
        kn = known[o["eng"]]
        o["deps"] = []
        for j in sorted(deps, reverse=True):
            src = ops[j]["dma"] or ops[j]["eng"]
            if kn.get(src, -1) >= j:
                continue
            o["deps"].append(j)
            need.add(j)
            kn[src] = j
            for s, k in ops[j]["clock"].items():
                if kn.get(s, -1) < k:
                    kn[s] = k
        o["clock"] = dict(kn)
        for name, m in o["w"]:
            h = [x for x in hist.get(name, []) if x[1] & ~m or SCRATCH[name][0] == "psum"]
            hist[name] = h + [(i, m, True)]
        for name, m in o["r"]:
            hist.setdefault(name, []).append((i, m, False))
    count = {e: 0 for e in q}
    waited = set()
    for i, o in enumerate(ops):
        e = q[o["eng"]]
        for s, n in o["waits"]:
            e.wait_ge(T.sem[s], n)
        for j in o["deps"]:
            if ops[j]["dma"]:
                e.wait_ge(T.sem[ops[j]["dma"]], 16)
                waited.add(j)
            else:
                e.wait_ge(T.sem["e" + ops[j]["eng"]], ops[j]["at"])
        ins = o["fn"](e)
        if o["dma"]:
            ins.then_inc(T.sem[o["dma"]], 16)
        elif i in need:
            count[o["eng"]] += 1
            o["at"] = count[o["eng"]]
            ins.then_inc(T.sem["e" + o["eng"]], 1)
    for i, o in enumerate(ops):
        if o["dma"] and i not in waited:
            q[o["eng"]].wait_ge(T.sem[o["dma"]], 16)
    g.wait_ge(T.sem.snt, sent)
